import numpy as np
import ml_dtypes


def mxq(x, axis, fmt="e4m3"):
    dtype, down = {"e4m3": (ml_dtypes.float8_e4m3fn, 7), "e5m2": (ml_dtypes.float8_e5m2, 14)}[fmt]
    v = np.moveaxis(np.asarray(x, np.float32).astype(ml_dtypes.bfloat16).astype(np.float64), axis, -1)
    blocks = v.reshape(v.shape[:-1] + (-1, 32))
    amax = np.abs(blocks).max(-1, keepdims=True)
    byte = np.maximum(np.where(amax > 0, np.frexp(amax)[1] - 1 + 127, 0) - down, 1)
    scale = np.exp2(byte - 127.0)
    codes = (blocks / scale).astype(np.float32).astype(dtype).astype(np.float64)
    return np.moveaxis((codes * scale).reshape(v.shape), -1, axis)


WIDE = False


def mx_kscale(k):
    if not WIDE:
        return np.ones(k)
    levels = np.array([30, -30])
    if k % 512:
        return np.exp2(np.random.permutation(np.resize(levels, k // 32))).repeat(32)
    a = np.empty((k // 512, 16))
    for p in range(k // 512):
        a[p, :8] = np.random.permutation(np.resize(levels, 8))
        for g in range(8):
            far = levels[np.abs(levels - a[p, g]) >= 10]
            a[p, g + 8] = far[np.random.randint(len(far))]
    return np.exp2(a.ravel()).repeat(32)


def f64(x):
    return np.asarray(x).astype(np.float64)


def striped(idx):
    return np.tile(idx.reshape(-1, 16).T, (8, 1)).astype(np.uint16)


def unstriped(offs):
    return offs[:16].T.reshape(-1).astype(np.int64)


def bf(x):
    return np.asarray(x, np.float32).astype(ml_dtypes.bfloat16)


E2M1 = np.array([0.0, 0.5, 1.0, 1.5, 2.0, 3.0, 4.0, 6.0, -0.0, -0.5, -1.0, -1.5, -2.0, -3.0, -4.0, -6.0])


def pack_weight(w, fmt):
    k, n = w.shape
    w = f64(bf(w)).reshape(k // 32, 32, n)
    amax = np.abs(w).max(1)
    if fmt in ("e4m3", "e5m2"):
        byte = np.frexp(amax)[1] - 1 + 127 - (7 if fmt == "e4m3" else 14)
    else:
        mant, ex = np.frexp(amax / 6.0)
        byte = np.where(mant > 0.5, ex, ex - 1) + 127
    byte = np.clip(np.where(amax > 0, byte, 1), 1, 254)
    scaled = (w * np.exp2(127.0 - byte)[:, None, :]).reshape(k, n).astype(np.float32)
    by_word = np.ascontiguousarray(scaled.reshape(k // 512, 128, 4, n).transpose(0, 1, 3, 2))
    if fmt in ("e4m3", "e5m2"):
        words = by_word.astype(ml_dtypes.float8_e4m3fn if fmt == "e4m3" else ml_dtypes.float8_e5m2).view(np.uint8)
    else:
        c = by_word.astype(ml_dtypes.float4_e2m1fn).view(np.uint8) & 0xF
        words = c[..., 0::2] | (c[..., 1::2] << 4)
    return np.ascontiguousarray(words), np.ascontiguousarray(byte.astype(np.uint8).reshape(k // 512, 16, n))


def unpack_weight(words, scales, fmt):
    g, p, n, _ = words.shape
    if fmt in ("e4m3", "e5m2"):
        vals = np.ascontiguousarray(words).view(ml_dtypes.float8_e4m3fn if fmt == "e4m3" else ml_dtypes.float8_e5m2).astype(np.float64)
    else:
        nib = np.empty((g, p, n, 4), np.uint8)
        nib[..., 0::2] = words & 0xF
        nib[..., 1::2] = words >> 4
        vals = E2M1[nib]
    vals = vals * np.repeat(np.exp2(scales.astype(np.float64) - 127.0), 8, axis=1)[..., None]
    return vals.transpose(0, 1, 3, 2).reshape(g * 512, n)


K, T, S, H, N, T2 = 1024, 2048, 1024, 1024, 512, 2048

def setup_inputs():
    n = np.random.standard_normal
    s = mx_kscale(K)[:, None]
    u = mx_kscale(H)[:, None]
    tab_words, tab_scales = pack_weight(n((K, T)) * np.exp(1.0 * n((1, T))) * s, "e5m2")
    wb_words, wb_scales = pack_weight(n((K, H)) / np.sqrt(K) / s * u.T, "e4m3")
    return {
        "tab_words": tab_words, "tab_scales": tab_scales,
        "offs": striped(np.random.permutation(T)[:S]),
        "wa": (n((K, H)) / np.sqrt(K) / s * u.T).astype(np.float32),
        "wb_words": wb_words, "wb_scales": wb_scales,
        "sT": (1.0 / (1.0 + np.exp(-n((H, T))))).astype(np.float32),
        "w3": (4.0 * n((H, N)) / np.sqrt(H) / u).astype(np.float32),
        "wgo": np.exp(0.3 * n((128, S))).astype(np.float32),
        "offs2": striped(np.random.permutation(T2)[:S]),
    }

def reference(tab_words, tab_scales, offs, wa, wb_words, wb_scales, sT, w3, wgo, offs2):
    v = unpack_weight(tab_words, tab_scales, "e5m2")[:, unstriped(offs)]
    a = mxq(f64(wa), 0, "e4m3").T @ v
    b = unpack_weight(wb_words, wb_scales, "e4m3").T @ v
    s_ = f64(sT)[:, unstriped(offs)]
    slope = s_ * (1.0 - s_)
    h = np.abs(a - b) * slope
    y = mxq(f64(w3), 0, "e4m3").T @ mxq(h, 0, "e4m3")
    out = np.zeros((N, T2))
    out[:, unstriped(offs2)] = np.tile(f64(wgo), (N // 128, 1)) * y
    return out

@@ -1,0 +1,266 @@
+from contextlib import ExitStack
+
+import concourse.mybir as mybir
+
+K, T, S, H, N, T2 = 1024, 2048, 1024, 1024, 512, 2048
+FLOPS = 2 * (2 * K * H * S + H * N * S)
+
+F32 = mybir.dt.float32
+BF16 = mybir.dt.bfloat16
+I32 = mybir.dt.int32
+U32 = mybir.dt.uint32
+U16 = mybir.dt.uint16
+U8 = mybir.dt.uint8
+E4 = mybir.dt.float8_e4m3fn_x4
+E5 = mybir.dt.float8_e5m2_x4
+ALU = mybir.AluOpType
+ACT = mybir.ActivationFunctionType
+
+P = 128
+PACK = 4
+PASS = P * PACK
+HALF = 512
+STREAM_BUFS = 9
+Y_BUFS = 4
+
+
+def tile_list_advisor_disagreement_audit_kernel(
+    tc, tab_words, tab_scales, offs, wa, wb_words, wb_scales, sT, w3, wgo, offs2, out
+):
+    nc = tc.nc
+    with ExitStack() as ctx:
+        lists = ctx.enter_context(tc.tile_pool(name="lists", bufs=1))
+        keep = ctx.enter_context(tc.tile_pool(name="keep", bufs=1))
+        psum = ctx.enter_context(tc.psum_pool(name="psum", bufs=8))
+
+        idx = lists.tile([P, S // 16], U16, name="idx")
+        idx2 = lists.tile([P, S // 16], U16, name="idx2")
+
+        def stream(shape, dtype, name):
+            return keep.tile(shape, dtype, name=name, tag="stream", bufs=STREAM_BUFS, align_bytes=64)
+
+        def woven(name, tag):
+            return keep.tile([P, PASS, PACK], BF16, name=name, tag=tag, bufs=2, align_bytes=64)
+
+        def held(shape, dtype, name):
+            return keep.tile(shape, dtype, name=name, align_bytes=64)
+
+        def half_list(lst, hf):
+            return lst[:, hf * (HALF // 16) : (hf + 1) * (HALF // 16)]
+
+        tab_plane = held([P, T], U8, "tab_plane")
+        wb_plane = stream([P, 2, H], U8, "wb_plane")
+        v_scales = [held([P, S], U8, "v_scales%d" % a) for a in range(2)]
+        nc.gpsimd.memset(tab_plane[:].bitcast(I32), 0)
+        nc.gpsimd.memset(v_scales[1][:].bitcast(I32), 0)
+        nc.gpsimd.memset(wb_plane[:].bitcast(I32), 0)
+        pages = [held([P, T2], F32, "page%d" % n) for n in range(N // P)]
+        for page in pages:
+            nc.gpsimd.memset(page[:], 0.0)
+
+        nc.sync.dma_start(idx[:], offs)
+        for q in range(4):
+            nc.sync.dma_start(
+                out=tab_plane[32 * q : 32 * q + 8, :].bitcast(I32), in_=tab_scales[:, 4 * q : 4 * q + 4, :].bitcast(I32)
+            )
+        tab = [stream([P, T], I32, "tab%d" % a) for a in range(2)]
+        for a in range(2):
+            nc.sync.dma_start(out=tab[a][:], in_=tab_words[a].rearrange("p t i -> p (t i)").bitcast(I32))
+        v_words = [held([P, S], U32, "v_words%d" % a) for a in range(2)]
+        nc.vector.tensor_copy(v_scales[0][:], tab_plane[:].indirect(idx[:]))
+        nc.sync.dma_start(out=v_scales[1][0:100, :].bitcast(I32), in_=v_scales[0][4:104, :].bitcast(I32))
+        for a in range(2):
+            nc.vector.tensor_copy(v_words[a][:], tab[a][:].bitcast(U32).indirect(idx[:]))
+
+        def r_rows(x, b, t):
+            return x[PASS * b : PASS * (b + 1), :].rearrange("(q t i) c -> t q i c", t=PACK, i=8)[t]
+
+        s_rows = {}
+
+        def load_s(b, t):
+            rows = stream([P, T], F32, "s_rows%d_%d" % (b, t))
+            nc.sync.dma_start(out=rows[:], in_=r_rows(sT, b, t))
+            s_rows[b, t] = rows
+
+        wa_codes, wa_scales = {}, {}
+
+        def quantise_wa(b, passes):
+            for a in passes:
+                raw = stream([P, PACK, PASS], F32, "wa_raw%d_%d" % (b, a))
+                nc.sync.dma_start(
+                    out=raw[:],
+                    in_=wa[PASS * a : PASS * (a + 1), PASS * b : PASS * (b + 1)].rearrange("(p i) c -> p i c", i=PACK),
+                )
+                w = woven("wa_woven%d_%d" % (b, a), "woven_w")
+                for t in range(PACK):
+                    nc.scalar.activation(
+                        out=w[:].rearrange("p (t q i) k -> p t q k i", t=PACK, i=8)[:, t],
+                        in_=raw[:].rearrange("p k (q t i) -> p t q k i", t=PACK, i=8)[:, t],
+                        func=ACT.Copy,
+                        scale=-1.0,
+                    )
+                wa_codes[b, a] = held([P, PASS], U32, "wa_codes%d_%d" % (b, a))
+                wa_scales[b, a] = held([P, PASS], U8, "wa_scales%d_%d" % (b, a))
+                nc.vector.quantize_mx(
+                    out=wa_codes[b, a][:].bitcast(E4), scales=wa_scales[b, a][:], in_=w[:].rearrange("p c i -> p (c i)")
+                )
+
+        def differences(b, hf):
+            banks = []
+            cols = slice(HALF * hf, HALF * (hf + 1))
+            for t in range(PACK):
+                bank = psum.tile([P, HALF], F32, name="d%d_%d_%d" % (b, hf, t), tag="bank")
+                m_wa = slice(P * t, P * (t + 1))
+                m_wb = slice(PASS * b + P * t, PASS * b + P * (t + 1))
+                passes = []
+                for a in range(2):
+                    passes.append((wb_codes[b][:, a, m_wa], wb_sc[:, a, m_wb], a))
+                for a in range(2):
+                    passes.append((wa_codes[b, a][:, m_wa], wa_scales[b, a][:, m_wa], a))
+                for i, (codes, scales, a) in enumerate(passes):
+                    nc.tensor.matmul_mx(
+                        out=bank[:],
+                        lhsT=codes.bitcast(E4),
+                        lhsT_scale=scales,
+                        rhs=v_words[a][:, cols].bitcast(E5),
+                        rhs_scale=v_scales[a][:, cols],
+                        start=(i == 0),
+                        stop=(i == len(passes) - 1),
+                    )
+                banks.append(bank)
+            return banks
+
+        h_codes, h_scales = {}, {}
+
+        def weigh(bank, s, u, second):
+            nc.vector.scalar_tensor_tensor(out=u, in0=s, scalar=1.0, in1=bank[:], op0=ALU.subtract, op1=ALU.mult)
+            second.tensor_tensor(out=u, in0=u, in1=s, op=ALU.mult)
+
+        def interleave(dst, src, func):
+            nc.scalar.activation(
+                out=dst[:].rearrange("p (c e) t -> p c t e", e=4),
+                in_=src[:].rearrange("p t (c e) -> p c t e", e=4),
+                func=func,
+            )
+
+        def quantise_h(b, hf, u):
+            w = woven("h_woven%d_%d" % (b, hf), "woven_h")
+            interleave(w, u, ACT.Abs)
+            h_codes[b, hf] = held([P, HALF], U32, "h_codes%d_%d" % (b, hf))
+            h_scales[b, hf] = held([P, HALF], U8, "h_scales%d_%d" % (b, hf))
+            nc.vector.quantize_mx(
+                out=h_codes[b, hf][:].bitcast(E4), scales=h_scales[b, hf][:], in_=w[:].rearrange("p c i -> p (c i)")
+            )
+
+        def gather_s(b, t, dst):
+            load_s(b, t)
+            nc.vector.tensor_copy(dst, s_rows[b, t][:].indirect(idx[:]))
+
+        w3_codes, w3_scales = [], []
+
+        def quantise_w3(b):
+            raw = stream([P, PACK, N], F32, "w3_raw%d" % b)
+            for t in range(PACK):
+                nc.sync.dma_start(out=raw[:, t, :], in_=r_rows(w3, b, t))
+            w = woven("w3_woven%d" % b, "woven_w")
+            interleave(w, raw, ACT.Copy)
+            w3_codes.append(held([P, N], U32, "w3_codes%d" % b))
+            w3_scales.append(held([P, N], U8, "w3_scales%d" % b))
+            nc.vector.quantize_mx(
+                out=w3_codes[b][:].bitcast(E4), scales=w3_scales[b][:], in_=w[:].rearrange("p c i -> p (c i)")
+            )
+
+        def load_wb_scale_rows(q):
+            nc.sync.dma_start(
+                out=wb_plane[32 * q : 32 * q + 4, :, :].bitcast(I32),
+                in_=wb_scales[:, 4 * q : 4 * q + 4, :].rearrange("a r c -> r a c").bitcast(I32),
+            )
+
+        wb_codes = {}
+
+        def order_wb(b):
+            raw = stream([P, 2, PASS], I32, "wb_raw%d" % b)
+            nc.sync.dma_start(
+                out=raw[:], in_=wb_words[:, :, PASS * b : PASS * (b + 1), :].rearrange("a p c i -> p a (c i)").bitcast(I32)
+            )
+            wb_codes[b] = held([P, 2, PASS], I32, "wb_codes%d" % b)
+            nc.vector.tensor_copy(
+                out=wb_codes[b][:].rearrange("p a (t q i) -> p a t q i", t=PACK, i=8),
+                in_=raw[:].rearrange("p a (q t i) -> p a t q i", t=PACK, i=8),
+            )
+
+        s0 = held([P, PACK, S], F32, "s0")
+        s1_early = held([P, 2, S], F32, "s1_early")
+        gather_s(0, 0, s0[:, 0, :])
+        load_wb_scale_rows(0)
+        quantise_wa(0, [0])
+        load_wb_scale_rows(1)
+        gather_s(0, 1, s0[:, 1, :])
+        load_wb_scale_rows(2)
+        quantise_wa(0, [1])
+        load_wb_scale_rows(3)
+        order_wb(0)
+        wb_sc = held([P, 2, H], U8, "wb_sc")
+        nc.vector.tensor_copy(
+            out=wb_sc[:].bitcast(I32).rearrange("p a (b t q i) -> p (a b) t q i", b=2, t=PACK, i=2),
+            in_=wb_plane[:].bitcast(I32).rearrange("p a (b q t i) -> p (a b) t q i", b=2, t=PACK, i=2),
+        )
+        gather_s(0, 2, s0[:, 2, :])
+        gather_s(0, 3, s0[:, 3, :])
+        quantise_wa(1, [0, 1])
+        order_wb(1)
+        for hf in range(2):
+            banks = differences(0, hf)
+            u = held([P, PACK, HALF], F32, "u0_%d" % hf)
+            for t in range(PACK):
+                weigh(banks[t], s0[:, t, HALF * hf : HALF * (hf + 1)], u[:, t, :], nc.gpsimd)
+            quantise_h(0, hf, u)
+
+        gather_s(1, 0, s1_early[:, 0, :])
+        gather_s(1, 1, s1_early[:, 1, :])
+        quantise_w3(0)
+        quantise_w3(1)
+        load_s(1, 2)
+        load_s(1, 3)
+        nc.sync.dma_start(idx2[:], offs2)
+        gains = stream([P, S], F32, "gains")
+        nc.sync.dma_start(out=gains[:], in_=wgo)
+
+        def late(shape, name):
+            return keep.tile(shape, F32, name=name, tag="late", bufs=1, align_bytes=64)
+
+        for hf in range(2):
+            banks = differences(1, hf)
+            s1 = keep.tile([P, 2, HALF], F32, name="s1_%d" % hf, tag="s1", bufs=1, align_bytes=64)
+            u = late([P, PACK, HALF], "u1_%d" % hf)
+            for t in range(2):
+                weigh(banks[t], s1_early[:, t, HALF * hf : HALF * (hf + 1)], u[:, t, :], nc.gpsimd)
+            for t in range(2, PACK):
+                nc.vector.tensor_copy(s1[:, t - 2, :], s_rows[1, t][:].indirect(half_list(idx, hf)))
+                last = hf == 0 and t == PACK - 1
+                weigh(banks[t], s1[:, t - 2, :], u[:, t, :], nc.vector if last else nc.gpsimd)
+            quantise_h(1, hf, u)
+
+        for hf in range(2):
+            for n in range(N // P):
+                bank = psum.tile([P, HALF], F32, name="y%d_%d" % (hf, n), tag="bank")
+                for b in range(2):
+                    nc.tensor.matmul_mx(
+                        out=bank[:],
+                        lhsT=w3_codes[b][:, P * n : P * (n + 1)].bitcast(E4),
+                        lhsT_scale=w3_scales[b][:, P * n : P * (n + 1)],
+                        rhs=h_codes[b, hf][:].bitcast(E4),
+                        rhs_scale=h_scales[b, hf][:],
+                        start=(b == 0),
+                        stop=(b == 1),
+                    )
+                if hf == 0 and n == N // P - 1:
+                    y = late([P, HALF], "y_late")
+                else:
+                    y = keep.tile([P, HALF], F32, name="y_sb%d_%d" % (hf, n), tag="y", bufs=Y_BUFS, align_bytes=64)
+                nc.scalar.copy(out=y[:], in_=bank[:])
+                nc.vector.tensor_tensor(
+                    pages[n][:].indirect(half_list(idx2, hf)), y[:], gains[:, HALF * hf : HALF * (hf + 1)], ALU.mult
+                )
+                if hf == 1:
+                    nc.sync.dma_start(out=out[P * n : P * (n + 1), :], in_=pages[n][:])

@@ -94,8 +94,8 @@ def tile_list_advisor_disagreement_audit_kernel(
                 w = woven("wa_woven%d_%d" % (b, a), "woven_w")
                 for t in range(PACK):
                     nc.scalar.activation(
-                        out=w[:].rearrange("p (t q i) k -> p t q k i", t=PACK, i=8)[:, t],
-                        in_=raw[:].rearrange("p k (q t i) -> p t q k i", t=PACK, i=8)[:, t],
+                        out=w[:].rearrange("p (t q i) k -> p t q i k", t=PACK, i=8)[:, t],
+                        in_=raw[:].rearrange("p k (q t i) -> p t q i k", t=PACK, i=8)[:, t],
                         func=ACT.Copy,
                         scale=-1.0,
                     )
@@ -138,8 +138,8 @@ def tile_list_advisor_disagreement_audit_kernel(
 
         def interleave(dst, src, func):
             nc.scalar.activation(
-                out=dst[:].rearrange("p (c e) t -> p c t e", e=4),
-                in_=src[:].rearrange("p t (c e) -> p c t e", e=4),
+                out=dst[:],
+                in_=src[:].rearrange("p t c -> p c t"),
                 func=func,
             )
 

@@ -55,8 +55,6 @@ def tile_list_advisor_disagreement_audit_kernel(
         nc.gpsimd.memset(v_scales[1][:].bitcast(I32), 0)
         nc.gpsimd.memset(wb_plane[:].bitcast(I32), 0)
         pages = [held([P, T2], F32, "page%d" % n) for n in range(N // P)]
-        for page in pages:
-            nc.gpsimd.memset(page[:], 0.0)
 
         nc.sync.dma_start(idx[:], offs)
         for q in range(4):
@@ -71,6 +69,9 @@ def tile_list_advisor_disagreement_audit_kernel(
         nc.sync.dma_start(out=v_scales[1][0:100, :].bitcast(I32), in_=v_scales[0][4:104, :].bitcast(I32))
         for a in range(2):
             nc.vector.tensor_copy(v_words[a][:], tab[a][:].bitcast(U32).indirect(idx[:]))
+
+        for page in pages:
+            nc.gpsimd.memset(page[:], 0.0)
 
         def r_rows(x, b, t):
             return x[PASS * b : PASS * (b + 1), :].rearrange("(q t i) c -> t q i c", t=PACK, i=8)[t]
@@ -132,9 +133,12 @@ def tile_list_advisor_disagreement_audit_kernel(
 
         h_codes, h_scales = {}, {}
 
-        def weigh(bank, s, u, second):
-            nc.vector.scalar_tensor_tensor(out=u, in0=s, scalar=1.0, in1=bank[:], op0=ALU.subtract, op1=ALU.mult)
-            second.tensor_tensor(out=u, in0=u, in1=s, op=ALU.mult)
+        def gather_slope(dst, rows, entries):
+            nc.vector.tensor_copy(dst, rows[:].indirect(entries))
+            nc.vector.scalar_tensor_tensor(out=dst, in0=dst, scalar=1.0, in1=dst, op0=ALU.subtract, op1=ALU.mult)
+
+        def weigh(bank, slope, u):
+            nc.vector.tensor_tensor(out=u, in0=bank[:], in1=slope, op=ALU.mult)
 
         def interleave(dst, src, func):
             nc.scalar.activation(
@@ -154,7 +158,7 @@ def tile_list_advisor_disagreement_audit_kernel(
 
         def gather_s(b, t, dst):
             load_s(b, t)
-            nc.vector.tensor_copy(dst, s_rows[b, t][:].indirect(idx[:]))
+            gather_slope(dst, s_rows[b, t], idx[:])
 
         w3_codes, w3_scales = [], []
 
@@ -213,7 +217,7 @@ def tile_list_advisor_disagreement_audit_kernel(
             banks = differences(0, hf)
             u = held([P, PACK, HALF], F32, "u0_%d" % hf)
             for t in range(PACK):
-                weigh(banks[t], s0[:, t, HALF * hf : HALF * (hf + 1)], u[:, t, :], nc.gpsimd)
+                weigh(banks[t], s0[:, t, HALF * hf : HALF * (hf + 1)], u[:, t, :])
             quantise_h(0, hf, u)
 
         gather_s(1, 0, s1_early[:, 0, :])
@@ -234,11 +238,10 @@ def tile_list_advisor_disagreement_audit_kernel(
             s1 = keep.tile([P, 2, HALF], F32, name="s1_%d" % hf, tag="s1", bufs=1, align_bytes=64)
             u = late([P, PACK, HALF], "u1_%d" % hf)
             for t in range(2):
-                weigh(banks[t], s1_early[:, t, HALF * hf : HALF * (hf + 1)], u[:, t, :], nc.gpsimd)
+                weigh(banks[t], s1_early[:, t, HALF * hf : HALF * (hf + 1)], u[:, t, :])
             for t in range(2, PACK):
-                nc.vector.tensor_copy(s1[:, t - 2, :], s_rows[1, t][:].indirect(half_list(idx, hf)))
-                last = hf == 0 and t == PACK - 1
-                weigh(banks[t], s1[:, t - 2, :], u[:, t, :], nc.vector if last else nc.gpsimd)
+                gather_slope(s1[:, t - 2, :], s_rows[1, t], half_list(idx, hf))
+                weigh(banks[t], s1[:, t - 2, :], u[:, t, :])
             quantise_h(1, hf, u)
 
         for hf in range(2):

@@ -74,7 +74,7 @@ def tile_list_advisor_disagreement_audit_kernel(
             nc.gpsimd.memset(page[:], 0.0)
 
         def r_rows(x, b, t):
-            return x[PASS * b : PASS * (b + 1), :].rearrange("(q t i) c -> t q i c", t=PACK, i=8)[t]
+            return x[PASS * b : PASS * (b + 1), :].rearrange("(p t) c -> p t c", t=PACK)[:, t, :]
 
         s_rows = {}
 
@@ -93,13 +93,12 @@ def tile_list_advisor_disagreement_audit_kernel(
                     in_=wa[PASS * a : PASS * (a + 1), PASS * b : PASS * (b + 1)].rearrange("(p i) c -> p i c", i=PACK),
                 )
                 w = woven("wa_woven%d_%d" % (b, a), "woven_w")
-                for t in range(PACK):
-                    nc.scalar.activation(
-                        out=w[:].rearrange("p (t q i) k -> p t q i k", t=PACK, i=8)[:, t],
-                        in_=raw[:].rearrange("p k (q t i) -> p t q i k", t=PACK, i=8)[:, t],
-                        func=ACT.Copy,
-                        scale=-1.0,
-                    )
+                nc.scalar.activation(
+                    out=w[:].rearrange("p (t m) k -> p m t k", t=PACK),
+                    in_=raw[:].rearrange("p k (m t) -> p m t k", t=PACK),
+                    func=ACT.Copy,
+                    scale=-1.0,
+                )
                 wa_codes[b, a] = held([P, PASS], U32, "wa_codes%d_%d" % (b, a))
                 wa_scales[b, a] = held([P, PASS], U8, "wa_scales%d_%d" % (b, a))
                 nc.vector.quantize_mx(
@@ -164,8 +163,7 @@ def tile_list_advisor_disagreement_audit_kernel(
 
         def quantise_w3(b):
             raw = stream([P, PACK, N], F32, "w3_raw%d" % b)
-            for t in range(PACK):
-                nc.sync.dma_start(out=raw[:, t, :], in_=r_rows(w3, b, t))
+            nc.sync.dma_start(out=raw[:], in_=w3[PASS * b : PASS * (b + 1), :].rearrange("(p t) n -> p t n", t=PACK))
             w = woven("w3_woven%d" % b, "woven_w")
             interleave(w, raw, ACT.Copy)
             w3_codes.append(held([P, N], U32, "w3_codes%d" % b))
@@ -189,8 +187,8 @@ def tile_list_advisor_disagreement_audit_kernel(
             )
             wb_codes[b] = held([P, 2, PASS], I32, "wb_codes%d" % b)
             nc.vector.tensor_copy(
-                out=wb_codes[b][:].rearrange("p a (t q i) -> p a t q i", t=PACK, i=8),
-                in_=raw[:].rearrange("p a (q t i) -> p a t q i", t=PACK, i=8),
+                out=wb_codes[b][:].rearrange("p a (t m) -> p a m t", t=PACK),
+                in_=raw[:].rearrange("p a (m t) -> p a m t", t=PACK),
             )
 
         s0 = held([P, PACK, S], F32, "s0")
@@ -206,8 +204,8 @@ def tile_list_advisor_disagreement_audit_kernel(
         order_wb(0)
         wb_sc = held([P, 2, H], U8, "wb_sc")
         nc.vector.tensor_copy(
-            out=wb_sc[:].bitcast(I32).rearrange("p a (b t q i) -> p (a b) t q i", b=2, t=PACK, i=2),
-            in_=wb_plane[:].bitcast(I32).rearrange("p a (b q t i) -> p (a b) t q i", b=2, t=PACK, i=2),
+            out=wb_sc[:].rearrange("p a (b t m) -> p (a b) t m", b=2, t=PACK),
+            in_=wb_plane[:].rearrange("p a (b m t) -> p (a b) t m", b=2, t=PACK),
         )
         gather_s(0, 2, s0[:, 2, :])
         gather_s(0, 3, s0[:, 3, :])

@@ -11,8 +11,8 @@ I32 = mybir.dt.int32
 U32 = mybir.dt.uint32
 U16 = mybir.dt.uint16
 U8 = mybir.dt.uint8
-E4 = mybir.dt.float8_e4m3fn_x4
-E5 = mybir.dt.float8_e5m2_x4
+E4M3 = mybir.dt.float8_e4m3fn_x4
+E5M2 = mybir.dt.float8_e5m2_x4
 ALU = mybir.AluOpType
 ACT = mybir.ActivationFunctionType
 
@@ -20,8 +20,12 @@ P = 128
 PACK = 4
 PASS = P * PACK
 HALF = 512
+QUADRANTS = 4
+LIST_COLS = S // 16
 STREAM_BUFS = 9
-Y_BUFS = 4
+PICK_BUFS = 7
+AFTER_BUFS = 4
+Y_BUFS = 3
 
 
 def tile_list_advisor_disagreement_audit_kernel(
@@ -33,152 +37,92 @@ def tile_list_advisor_disagreement_audit_kernel(
         keep = ctx.enter_context(tc.tile_pool(name="keep", bufs=1))
         psum = ctx.enter_context(tc.psum_pool(name="psum", bufs=8))
 
-        idx = lists.tile([P, S // 16], U16, name="idx")
-        idx2 = lists.tile([P, S // 16], U16, name="idx2")
-
-        def stream(shape, dtype, name):
-            return keep.tile(shape, dtype, name=name, tag="stream", bufs=STREAM_BUFS, align_bytes=64)
-
-        def woven(name, tag):
-            return keep.tile([P, PASS, PACK], BF16, name=name, tag=tag, bufs=2, align_bytes=64)
-
         def held(shape, dtype, name):
             return keep.tile(shape, dtype, name=name, align_bytes=64)
 
+        def shared(shape, dtype, name, tag, bufs):
+            return keep.tile(shape, dtype, name=name, tag=tag, bufs=bufs, align_bytes=64)
+
+        def stream(shape, dtype, name):
+            return shared(shape, dtype, name, "stream", STREAM_BUFS)
+
+        def half_cols(hf):
+            return slice(HALF * hf, HALF * (hf + 1))
+
         def half_list(lst, hf):
-            return lst[:, hf * (HALF // 16) : (hf + 1) * (HALF // 16)]
+            return lst[:, LIST_COLS // 2 * hf : LIST_COLS // 2 * (hf + 1)]
+
+        def group_rows(x, b):
+            return x[PASS * b : PASS * (b + 1)].rearrange("(p t) c -> p t c", t=PACK)
+
+        def quantise(woven, name, tag, bufs):
+            codes = shared([P, PASS], U32, name + "_codes", tag, bufs)
+            plane = held([P, PASS], U8, name + "_plane")
+            nc.vector.quantize_mx(out=codes[:].bitcast(E4M3), scales=plane[:], in_=woven[:].rearrange("p c i -> p (c i)"))
+            return codes, plane
 
         tab_plane = held([P, T], U8, "tab_plane")
         wb_plane = stream([P, 2, H], U8, "wb_plane")
-        v_scales = [held([P, S], U8, "v_scales%d" % a) for a in range(2)]
+        v_planes = [held([P, S], U8, "v_plane%d" % a) for a in range(2)]
         nc.gpsimd.memset(tab_plane[:].bitcast(I32), 0)
-        nc.gpsimd.memset(v_scales[1][:].bitcast(I32), 0)
+        nc.gpsimd.memset(v_planes[1][:].bitcast(I32), 0)
         nc.gpsimd.memset(wb_plane[:].bitcast(I32), 0)
         pages = [held([P, T2], F32, "page%d" % n) for n in range(N // P)]
+        for page in pages:
+            nc.gpsimd.memset(page[:], 0.0)
 
+        idx = lists.tile([P, LIST_COLS], U16, name="idx")
         nc.sync.dma_start(idx[:], offs)
-        for q in range(4):
+        for q in range(QUADRANTS):
             nc.sync.dma_start(
                 out=tab_plane[32 * q : 32 * q + 8, :].bitcast(I32), in_=tab_scales[:, 4 * q : 4 * q + 4, :].bitcast(I32)
             )
         tab = [stream([P, T], I32, "tab%d" % a) for a in range(2)]
         for a in range(2):
             nc.sync.dma_start(out=tab[a][:], in_=tab_words[a].rearrange("p t i -> p (t i)").bitcast(I32))
+        nc.vector.tensor_copy(v_planes[0][:], tab_plane[:].indirect(idx[:]))
+        live = 32 * (QUADRANTS - 1) + 4
+        nc.sync.dma_start(out=v_planes[1][0:live, :].bitcast(I32), in_=v_planes[0][4 : live + 4, :].bitcast(I32))
         v_words = [held([P, S], U32, "v_words%d" % a) for a in range(2)]
-        nc.vector.tensor_copy(v_scales[0][:], tab_plane[:].indirect(idx[:]))
-        nc.sync.dma_start(out=v_scales[1][0:100, :].bitcast(I32), in_=v_scales[0][4:104, :].bitcast(I32))
         for a in range(2):
             nc.vector.tensor_copy(v_words[a][:], tab[a][:].bitcast(U32).indirect(idx[:]))
 
-        for page in pages:
-            nc.gpsimd.memset(page[:], 0.0)
-
-        def r_rows(x, b, t):
-            return x[PASS * b : PASS * (b + 1), :].rearrange("(p t) c -> p t c", t=PACK)[:, t, :]
-
-        s_rows = {}
+        s_rows, picked, slopes, wa_mx, wb_codes = {}, {}, {}, {}, {}
+        w3_woven, w3_mx, h_woven, h_mx = {}, {}, {}, {}
 
         def load_s(b, t):
-            rows = stream([P, T], F32, "s_rows%d_%d" % (b, t))
-            nc.sync.dma_start(out=rows[:], in_=r_rows(sT, b, t))
-            s_rows[b, t] = rows
+            s_rows[b, t] = stream([P, T], F32, "s_rows%d_%d" % (b, t))
+            nc.sync.dma_start(out=s_rows[b, t][:], in_=group_rows(sT, b)[:, t, :])
 
-        wa_codes, wa_scales = {}, {}
-
-        def quantise_wa(b, passes):
-            for a in passes:
-                raw = stream([P, PACK, PASS], F32, "wa_raw%d_%d" % (b, a))
-                nc.sync.dma_start(
-                    out=raw[:],
-                    in_=wa[PASS * a : PASS * (a + 1), PASS * b : PASS * (b + 1)].rearrange("(p i) c -> p i c", i=PACK),
-                )
-                w = woven("wa_woven%d_%d" % (b, a), "woven_w")
-                nc.scalar.activation(
-                    out=w[:].rearrange("p (t m) k -> p m t k", t=PACK),
-                    in_=raw[:].rearrange("p k (m t) -> p m t k", t=PACK),
-                    func=ACT.Copy,
-                    scale=-1.0,
-                )
-                wa_codes[b, a] = held([P, PASS], U32, "wa_codes%d_%d" % (b, a))
-                wa_scales[b, a] = held([P, PASS], U8, "wa_scales%d_%d" % (b, a))
-                nc.vector.quantize_mx(
-                    out=wa_codes[b, a][:].bitcast(E4), scales=wa_scales[b, a][:], in_=w[:].rearrange("p c i -> p (c i)")
-                )
-
-        def differences(b, hf):
-            banks = []
-            cols = slice(HALF * hf, HALF * (hf + 1))
-            for t in range(PACK):
-                bank = psum.tile([P, HALF], F32, name="d%d_%d_%d" % (b, hf, t), tag="bank")
-                m_wa = slice(P * t, P * (t + 1))
-                m_wb = slice(PASS * b + P * t, PASS * b + P * (t + 1))
-                passes = []
-                for a in range(2):
-                    passes.append((wb_codes[b][:, a, m_wa], wb_sc[:, a, m_wb], a))
-                for a in range(2):
-                    passes.append((wa_codes[b, a][:, m_wa], wa_scales[b, a][:, m_wa], a))
-                for i, (codes, scales, a) in enumerate(passes):
-                    nc.tensor.matmul_mx(
-                        out=bank[:],
-                        lhsT=codes.bitcast(E4),
-                        lhsT_scale=scales,
-                        rhs=v_words[a][:, cols].bitcast(E5),
-                        rhs_scale=v_scales[a][:, cols],
-                        start=(i == 0),
-                        stop=(i == len(passes) - 1),
-                    )
-                banks.append(bank)
-            return banks
-
-        h_codes, h_scales = {}, {}
-
-        def gather_slope(dst, rows, entries):
-            nc.vector.tensor_copy(dst, rows[:].indirect(entries))
-            nc.vector.scalar_tensor_tensor(out=dst, in0=dst, scalar=1.0, in1=dst, op0=ALU.subtract, op1=ALU.mult)
-
-        def weigh(bank, slope, u):
-            nc.vector.tensor_tensor(out=u, in0=bank[:], in1=slope, op=ALU.mult)
-
-        def interleave(dst, src, func):
-            nc.scalar.activation(
-                out=dst[:],
-                in_=src[:].rearrange("p t c -> p c t"),
-                func=func,
-            )
-
-        def quantise_h(b, hf, u):
-            w = woven("h_woven%d_%d" % (b, hf), "woven_h")
-            interleave(w, u, ACT.Abs)
-            h_codes[b, hf] = held([P, HALF], U32, "h_codes%d_%d" % (b, hf))
-            h_scales[b, hf] = held([P, HALF], U8, "h_scales%d_%d" % (b, hf))
-            nc.vector.quantize_mx(
-                out=h_codes[b, hf][:].bitcast(E4), scales=h_scales[b, hf][:], in_=w[:].rearrange("p c i -> p (c i)")
-            )
-
-        def gather_s(b, t, dst):
+        def pick(b, t):
             load_s(b, t)
-            gather_slope(dst, s_rows[b, t], idx[:])
+            picked[b, t] = shared([P, S], F32, "picked%d_%d" % (b, t), "pick", PICK_BUFS)
+            nc.vector.tensor_copy(picked[b, t][:], s_rows[b, t][:].indirect(idx[:]))
 
-        w3_codes, w3_scales = [], []
+        def minus_slope(dst, s):
+            nc.vector.scalar_tensor_tensor(out=dst, in0=s, scalar=1.0, in1=s, op0=ALU.subtract, op1=ALU.mult)
 
-        def quantise_w3(b):
-            raw = stream([P, PACK, N], F32, "w3_raw%d" % b)
-            nc.sync.dma_start(out=raw[:], in_=w3[PASS * b : PASS * (b + 1), :].rearrange("(p t) n -> p t n", t=PACK))
-            w = woven("w3_woven%d" % b, "woven_w")
-            interleave(w, raw, ACT.Copy)
-            w3_codes.append(held([P, N], U32, "w3_codes%d" % b))
-            w3_scales.append(held([P, N], U8, "w3_scales%d" % b))
-            nc.vector.quantize_mx(
-                out=w3_codes[b][:].bitcast(E4), scales=w3_scales[b][:], in_=w[:].rearrange("p c i -> p (c i)")
+        def slope(b, t):
+            slopes[b, t] = shared([P, S], F32, "slope%d_%d" % (b, t), "pick", PICK_BUFS)
+            minus_slope(slopes[b, t][:], picked[b, t][:])
+
+        def quantise_wa(b, a):
+            raw = stream([P, PACK, PASS], F32, "wa_raw%d_%d" % (b, a))
+            nc.sync.dma_start(out=raw[:], in_=group_rows(wa[:, PASS * b : PASS * (b + 1)], a))
+            woven = shared([P, PASS, PACK], BF16, "wa_woven%d_%d" % (b, a), "woven_w", 2)
+            nc.scalar.activation(
+                out=woven[:].rearrange("p (t m) i -> p m t i", t=PACK),
+                in_=raw[:].rearrange("p i (m t) -> p m t i", t=PACK),
+                func=ACT.Copy,
+                scale=-1.0,
             )
+            wa_mx[b, a] = quantise(woven, "wa%d_%d" % (b, a), "wa_codes", 4)
 
         def load_wb_scale_rows(q):
             nc.sync.dma_start(
                 out=wb_plane[32 * q : 32 * q + 4, :, :].bitcast(I32),
                 in_=wb_scales[:, 4 * q : 4 * q + 4, :].rearrange("a r c -> r a c").bitcast(I32),
             )
-
-        wb_codes = {}
 
         def order_wb(b):
             raw = stream([P, 2, PASS], I32, "wb_raw%d" % b)
@@ -187,81 +131,130 @@ def tile_list_advisor_disagreement_audit_kernel(
             )
             wb_codes[b] = held([P, 2, PASS], I32, "wb_codes%d" % b)
             nc.vector.tensor_copy(
-                out=wb_codes[b][:].rearrange("p a (t m) -> p a m t", t=PACK),
-                in_=raw[:].rearrange("p a (m t) -> p a m t", t=PACK),
+                out=wb_codes[b][:].rearrange("p a (t g e) -> p a g t e", t=PACK, e=4),
+                in_=raw[:].rearrange("p a (g e t) -> p a g t e", t=PACK, e=4),
             )
 
-        s0 = held([P, PACK, S], F32, "s0")
-        s1_early = held([P, 2, S], F32, "s1_early")
-        gather_s(0, 0, s0[:, 0, :])
+        def interleave_w3(b):
+            raw = stream([P, PACK, N], F32, "w3_raw%d" % b)
+            nc.sync.dma_start(out=raw[:], in_=group_rows(w3, b))
+            woven = shared([P, N, PACK], BF16, "w3_woven%d" % b, "woven_w", 2)
+            nc.scalar.activation(out=woven[:], in_=raw[:].rearrange("p t n -> p n t"), func=ACT.Copy)
+            w3_woven[b] = woven
+
+        def differences(b, hf):
+            banks = []
+            for t in range(PACK):
+                bank = psum.tile([P, HALF], F32, name="d%d_%d_%d" % (b, hf, t), tag="bank")
+                cols = slice(P * t, P * (t + 1))
+                cols_of_all = slice(PASS * b + P * t, PASS * b + P * (t + 1))
+                passes = [(wb_codes[b][:, a, cols], wb_ordered_plane[:, a, cols_of_all], a) for a in range(2)]
+                passes = passes + [(wa_mx[b, a][0][:, cols], wa_mx[b, a][1][:, cols], a) for a in range(2)]
+                for number, (codes, plane, a) in enumerate(passes):
+                    nc.tensor.matmul_mx(
+                        out=bank[:],
+                        lhsT=codes.bitcast(E4M3),
+                        lhsT_scale=plane,
+                        rhs=v_words[a][:, half_cols(hf)].bitcast(E5M2),
+                        rhs_scale=v_planes[a][:, half_cols(hf)],
+                        start=(number == 0),
+                        stop=(number == len(passes) - 1),
+                    )
+                banks.append(bank)
+            return banks
+
+        def weigh(signed_h, bank, slope_part):
+            nc.vector.tensor_tensor(out=signed_h, in0=bank[:], in1=slope_part, op=ALU.mult)
+
+        def interleave_h(b, hf, signed_h):
+            h_woven[b, hf] = shared([P, HALF, PACK], BF16, "h_woven%d_%d" % (b, hf), "woven_h", 2)
+            nc.scalar.activation(out=h_woven[b, hf][:], in_=signed_h[:].rearrange("p t j -> p j t"), func=ACT.Abs)
+
+        def quantise_h(b, hf, tag, bufs):
+            h_mx[b, hf] = quantise(h_woven[b, hf], "h%d_%d" % (b, hf), tag, bufs)
+
+        pick(0, 0)
         load_wb_scale_rows(0)
-        quantise_wa(0, [0])
+        pick(0, 1)
+        slope(0, 0)
+        slope(0, 1)
         load_wb_scale_rows(1)
-        gather_s(0, 1, s0[:, 1, :])
+        quantise_wa(0, 0)
         load_wb_scale_rows(2)
-        quantise_wa(0, [1])
+        pick(0, 2)
+        quantise_wa(0, 1)
         load_wb_scale_rows(3)
         order_wb(0)
-        wb_sc = held([P, 2, H], U8, "wb_sc")
+        wb_ordered_plane = held([P, 2, H], U8, "wb_ordered_plane")
         nc.vector.tensor_copy(
-            out=wb_sc[:].rearrange("p a (b t m) -> p (a b) t m", b=2, t=PACK),
+            out=wb_ordered_plane[:].rearrange("p a (b t m) -> p (a b) t m", b=2, t=PACK),
             in_=wb_plane[:].rearrange("p a (b m t) -> p (a b) t m", b=2, t=PACK),
         )
-        gather_s(0, 2, s0[:, 2, :])
-        gather_s(0, 3, s0[:, 3, :])
-        quantise_wa(1, [0, 1])
+        pick(0, 3)
+        slope(0, 2)
+        slope(0, 3)
+        quantise_wa(1, 0)
+        quantise_wa(1, 1)
         order_wb(1)
         for hf in range(2):
             banks = differences(0, hf)
-            u = held([P, PACK, HALF], F32, "u0_%d" % hf)
+            signed_h = held([P, PACK, HALF], F32, "signed_h0_%d" % hf)
             for t in range(PACK):
-                weigh(banks[t], s0[:, t, HALF * hf : HALF * (hf + 1)], u[:, t, :])
-            quantise_h(0, hf, u)
+                weigh(signed_h[:, t, :], banks[t], slopes[0, t][:, half_cols(hf)])
+            interleave_h(0, hf, signed_h)
 
-        gather_s(1, 0, s1_early[:, 0, :])
-        gather_s(1, 1, s1_early[:, 1, :])
-        quantise_w3(0)
-        quantise_w3(1)
+        pick(1, 0)
+        pick(1, 1)
+        slope(1, 0)
+        slope(1, 1)
+        interleave_w3(0)
+        interleave_w3(1)
         load_s(1, 2)
         load_s(1, 3)
+        idx2 = lists.tile([P, LIST_COLS], U16, name="idx2")
         nc.sync.dma_start(idx2[:], offs2)
         gains = stream([P, S], F32, "gains")
         nc.sync.dma_start(out=gains[:], in_=wgo)
 
-        def late(shape, name):
-            return keep.tile(shape, F32, name=name, tag="late", bufs=1, align_bytes=64)
-
         for hf in range(2):
             banks = differences(1, hf)
-            s1 = keep.tile([P, 2, HALF], F32, name="s1_%d" % hf, tag="s1", bufs=1, align_bytes=64)
-            u = late([P, PACK, HALF], "u1_%d" % hf)
+            late_slopes = shared([P, 2, HALF], F32, "late_slopes%d" % hf, "after_slopes", AFTER_BUFS)
+            signed_h = shared([P, PACK, HALF], F32, "signed_h1_%d" % hf, "late", 1)
             for t in range(2):
-                weigh(banks[t], s1_early[:, t, HALF * hf : HALF * (hf + 1)], u[:, t, :])
+                weigh(signed_h[:, t, :], banks[t], slopes[1, t][:, half_cols(hf)])
             for t in range(2, PACK):
-                gather_slope(s1[:, t - 2, :], s_rows[1, t], half_list(idx, hf))
-                weigh(banks[t], s1[:, t - 2, :], u[:, t, :])
-            quantise_h(1, hf, u)
+                part = late_slopes[:, t - 2, :]
+                nc.vector.tensor_copy(part, s_rows[1, t][:].indirect(half_list(idx, hf)))
+                minus_slope(part, part)
+                weigh(signed_h[:, t, :], banks[t], part)
+            if hf == 0:
+                quantise_h(0, 0, "after_slopes", AFTER_BUFS)
+                for b in range(2):
+                    w3_mx[b] = quantise(w3_woven[b], "w3_%d" % b, "after_slopes", AFTER_BUFS)
+            interleave_h(1, hf, signed_h)
+            quantise_h(1, hf, "h_codes", 3)
+            if hf == 0:
+                quantise_h(0, 1, "h_codes", 3)
 
         for hf in range(2):
             for n in range(N // P):
                 bank = psum.tile([P, HALF], F32, name="y%d_%d" % (hf, n), tag="bank")
+                cols = slice(P * n, P * (n + 1))
                 for b in range(2):
                     nc.tensor.matmul_mx(
                         out=bank[:],
-                        lhsT=w3_codes[b][:, P * n : P * (n + 1)].bitcast(E4),
-                        lhsT_scale=w3_scales[b][:, P * n : P * (n + 1)],
-                        rhs=h_codes[b, hf][:].bitcast(E4),
-                        rhs_scale=h_scales[b, hf][:],
+                        lhsT=w3_mx[b][0][:, cols].bitcast(E4M3),
+                        lhsT_scale=w3_mx[b][1][:, cols],
+                        rhs=h_mx[b, hf][0][:].bitcast(E4M3),
+                        rhs_scale=h_mx[b, hf][1][:],
                         start=(b == 0),
                         stop=(b == 1),
                     )
                 if hf == 0 and n == N // P - 1:
-                    y = late([P, HALF], "y_late")
+                    y = shared([P, HALF], F32, "y_late", "late", 1)
                 else:
-                    y = keep.tile([P, HALF], F32, name="y_sb%d_%d" % (hf, n), tag="y", bufs=Y_BUFS, align_bytes=64)
+                    y = shared([P, HALF], F32, "y_sb%d_%d" % (hf, n), "y", Y_BUFS)
                 nc.scalar.copy(out=y[:], in_=bank[:])
-                nc.vector.tensor_tensor(
-                    pages[n][:].indirect(half_list(idx2, hf)), y[:], gains[:, HALF * hf : HALF * (hf + 1)], ALU.mult
-                )
+                nc.vector.tensor_tensor(pages[n][:].indirect(half_list(idx2, hf)), y[:], gains[:, half_cols(hf)], ALU.mult)
                 if hf == 1:
-                    nc.sync.dma_start(out=out[P * n : P * (n + 1), :], in_=pages[n][:])
+                    nc.sync.dma_start(out=out[cols, :], in_=pages[n][:])

@@ -23,9 +23,7 @@ HALF = 512
 QUADRANTS = 4
 LIST_COLS = S // 16
 STREAM_BUFS = 9
-PICK_BUFS = 7
-AFTER_BUFS = 4
-Y_BUFS = 3
+WORK_BUFS = 30
 
 
 def tile_list_advisor_disagreement_audit_kernel(
@@ -35,16 +33,16 @@ def tile_list_advisor_disagreement_audit_kernel(
     with ExitStack() as ctx:
         lists = ctx.enter_context(tc.tile_pool(name="lists", bufs=1))
         keep = ctx.enter_context(tc.tile_pool(name="keep", bufs=1))
-        psum = ctx.enter_context(tc.psum_pool(name="psum", bufs=8))
+        psum = ctx.enter_context(tc.psum_pool(name="psum", bufs=1))
 
         def held(shape, dtype, name):
             return keep.tile(shape, dtype, name=name, align_bytes=64)
 
-        def shared(shape, dtype, name, tag, bufs):
-            return keep.tile(shape, dtype, name=name, tag=tag, bufs=bufs, align_bytes=64)
-
         def stream(shape, dtype, name):
-            return shared(shape, dtype, name, "stream", STREAM_BUFS)
+            return keep.tile(shape, dtype, name=name, tag="stream", bufs=STREAM_BUFS, align_bytes=64)
+
+        def work(shape, dtype, name):
+            return keep.tile(shape, dtype, name=name, tag="work", bufs=WORK_BUFS, align_bytes=64)
 
         def half_cols(hf):
             return slice(HALF * hf, HALF * (hf + 1))
@@ -55,15 +53,15 @@ def tile_list_advisor_disagreement_audit_kernel(
         def group_rows(x, b):
             return x[PASS * b : PASS * (b + 1)].rearrange("(p t) c -> p t c", t=PACK)
 
-        def quantise(woven, name, tag, bufs):
-            codes = shared([P, PASS], U32, name + "_codes", tag, bufs)
+        def quantise(woven, name):
+            codes = work([P, PASS], U32, name + "_codes")
             plane = held([P, PASS], U8, name + "_plane")
-            nc.vector.quantize_mx(out=codes[:].bitcast(E4M3), scales=plane[:], in_=woven[:].rearrange("p c i -> p (c i)"))
+            nc.vector.quantize_mx(out=codes[:].bitcast(E4M3), scales=plane[:], in_=woven)
             return codes, plane
 
         tab_plane = held([P, T], U8, "tab_plane")
         wb_plane = stream([P, 2, H], U8, "wb_plane")
-        v_planes = [held([P, S], U8, "v_plane%d" % a) for a in range(2)]
+        v_planes = [work([P, S], U8, "v_plane0"), held([P, S], U8, "v_plane1")]
         nc.gpsimd.memset(tab_plane[:].bitcast(I32), 0)
         nc.gpsimd.memset(v_planes[1][:].bitcast(I32), 0)
         nc.gpsimd.memset(wb_plane[:].bitcast(I32), 0)
@@ -83,40 +81,47 @@ def tile_list_advisor_disagreement_audit_kernel(
         nc.vector.tensor_copy(v_planes[0][:], tab_plane[:].indirect(idx[:]))
         live = 32 * (QUADRANTS - 1) + 4
         nc.sync.dma_start(out=v_planes[1][0:live, :].bitcast(I32), in_=v_planes[0][4 : live + 4, :].bitcast(I32))
-        v_words = [held([P, S], U32, "v_words%d" % a) for a in range(2)]
+        v_words = [work([P, S], U32, "v_words%d" % a) for a in range(2)]
         for a in range(2):
             nc.vector.tensor_copy(v_words[a][:], tab[a][:].bitcast(U32).indirect(idx[:]))
 
-        s_rows, picked, slopes, wa_mx, wb_codes = {}, {}, {}, {}, {}
-        w3_woven, w3_mx, h_woven, h_mx = {}, {}, {}, {}
+        s_rows, picked, slopes, wa_woven, wa_mx, wb_codes, signed_h = {}, {}, {}, {}, {}, {}, {}
+        w3_raw, w3_woven, w3_mx, h_woven, h_mx = {}, {}, {}, {}, {}
 
         def load_s(b, t):
             s_rows[b, t] = stream([P, T], F32, "s_rows%d_%d" % (b, t))
             nc.sync.dma_start(out=s_rows[b, t][:], in_=group_rows(sT, b)[:, t, :])
 
-        def pick(b, t):
-            load_s(b, t)
-            picked[b, t] = shared([P, S], F32, "picked%d_%d" % (b, t), "pick", PICK_BUFS)
-            nc.vector.tensor_copy(picked[b, t][:], s_rows[b, t][:].indirect(idx[:]))
+        def pick(b, t, halves):
+            name = "%d_%d_%d" % (b, t, halves[0])
+            picked[b, t, halves] = work([P, HALF * len(halves)], F32, "picked" + name)
+            entries = idx[:] if len(halves) == 2 else half_list(idx, halves[0])
+            nc.vector.tensor_copy(picked[b, t, halves][:], s_rows[b, t][:].indirect(entries))
 
-        def minus_slope(dst, s):
-            nc.vector.scalar_tensor_tensor(out=dst, in0=s, scalar=1.0, in1=s, op0=ALU.subtract, op1=ALU.mult)
+        def slope(b, t, halves, on_vector):
+            s = picked[b, t, halves][:]
+            made = work([P, HALF * len(halves)], F32, "slope%d_%d_%d" % (b, t, halves[0]))
+            if on_vector:
+                nc.vector.scalar_tensor_tensor(out=made[:], in0=s, scalar=1.0, in1=s, op0=ALU.subtract, op1=ALU.mult)
+            else:
+                nc.scalar.activation(out=made[:], in_=s, func=ACT.Copy, scale=-1.0, bias=1.0)
+                nc.gpsimd.tensor_tensor(out=made[:], in0=made[:], in1=s, op=ALU.mult)
+            for place, hf in enumerate(halves):
+                slopes[b, t, hf] = made[:, half_cols(place)]
 
-        def slope(b, t):
-            slopes[b, t] = shared([P, S], F32, "slope%d_%d" % (b, t), "pick", PICK_BUFS)
-            minus_slope(slopes[b, t][:], picked[b, t][:])
-
-        def quantise_wa(b, a):
+        def weave_wa(b, a):
             raw = stream([P, PACK, PASS], F32, "wa_raw%d_%d" % (b, a))
             nc.sync.dma_start(out=raw[:], in_=group_rows(wa[:, PASS * b : PASS * (b + 1)], a))
-            woven = shared([P, PASS, PACK], BF16, "wa_woven%d_%d" % (b, a), "woven_w", 2)
+            wa_woven[b, a] = work([P, PASS, PACK], BF16, "wa_woven%d_%d" % (b, a))
             nc.scalar.activation(
-                out=woven[:].rearrange("p (t m) i -> p m t i", t=PACK),
+                out=wa_woven[b, a][:].rearrange("p (t m) i -> p m t i", t=PACK),
                 in_=raw[:].rearrange("p i (m t) -> p m t i", t=PACK),
                 func=ACT.Copy,
                 scale=-1.0,
             )
-            wa_mx[b, a] = quantise(woven, "wa%d_%d" % (b, a), "wa_codes", 4)
+
+        def quantise_wa(b, a):
+            wa_mx[b, a] = quantise(wa_woven[b, a][:].rearrange("p c i -> p (c i)"), "wa%d_%d" % (b, a))
 
         def load_wb_scale_rows(q):
             nc.sync.dma_start(
@@ -124,137 +129,165 @@ def tile_list_advisor_disagreement_audit_kernel(
                 in_=wb_scales[:, 4 * q : 4 * q + 4, :].rearrange("a r c -> r a c").bitcast(I32),
             )
 
-        def order_wb(b):
-            raw = stream([P, 2, PASS], I32, "wb_raw%d" % b)
-            nc.sync.dma_start(
-                out=raw[:], in_=wb_words[:, :, PASS * b : PASS * (b + 1), :].rearrange("a p c i -> p a (c i)").bitcast(I32)
-            )
-            wb_codes[b] = held([P, 2, PASS], I32, "wb_codes%d" % b)
+        def load_wb():
+            raw = stream([P, 2, H], I32, "wb_raw")
+            nc.sync.dma_start(out=raw[:], in_=wb_words.rearrange("a p c i -> p a (c i)").bitcast(I32))
+            return raw
+
+        def order_wb(raw, a):
+            wb_codes[a] = work([P, H], I32, "wb_codes%d" % a)
             nc.vector.tensor_copy(
-                out=wb_codes[b][:].rearrange("p a (t g e) -> p a g t e", t=PACK, e=4),
-                in_=raw[:].rearrange("p a (g e t) -> p a g t e", t=PACK, e=4),
+                out=wb_codes[a][:].rearrange("p (b t g e) -> p b g t e", b=2, t=PACK, e=4),
+                in_=raw[:, a, :].rearrange("p (b g e t) -> p b g t e", b=2, t=PACK, e=4),
             )
 
-        def interleave_w3(b):
-            raw = stream([P, PACK, N], F32, "w3_raw%d" % b)
-            nc.sync.dma_start(out=raw[:], in_=group_rows(w3, b))
-            woven = shared([P, N, PACK], BF16, "w3_woven%d" % b, "woven_w", 2)
-            nc.scalar.activation(out=woven[:], in_=raw[:].rearrange("p t n -> p n t"), func=ACT.Copy)
-            w3_woven[b] = woven
+        def order_wb_plane():
+            ordered = work([P, 2, H], U8, "wb_ordered_plane")
+            nc.vector.tensor_copy(
+                out=ordered[:].rearrange("p a (b t m) -> p (a b) t m", b=2, t=PACK),
+                in_=wb_plane[:].rearrange("p a (b m t) -> p (a b) t m", b=2, t=PACK),
+            )
+            return ordered
 
-        def differences(b, hf):
-            banks = []
-            for t in range(PACK):
-                bank = psum.tile([P, HALF], F32, name="d%d_%d_%d" % (b, hf, t), tag="bank")
-                cols = slice(P * t, P * (t + 1))
-                cols_of_all = slice(PASS * b + P * t, PASS * b + P * (t + 1))
-                passes = [(wb_codes[b][:, a, cols], wb_ordered_plane[:, a, cols_of_all], a) for a in range(2)]
-                passes = passes + [(wa_mx[b, a][0][:, cols], wa_mx[b, a][1][:, cols], a) for a in range(2)]
-                for number, (codes, plane, a) in enumerate(passes):
-                    nc.tensor.matmul_mx(
-                        out=bank[:],
-                        lhsT=codes.bitcast(E4M3),
-                        lhsT_scale=plane,
-                        rhs=v_words[a][:, half_cols(hf)].bitcast(E5M2),
-                        rhs_scale=v_planes[a][:, half_cols(hf)],
-                        start=(number == 0),
-                        stop=(number == len(passes) - 1),
-                    )
-                banks.append(bank)
-            return banks
+        def load_w3(c):
+            w3_raw[c] = stream([P, 2, PACK, N // 2], F32, "w3_raw%d" % c)
+            for b in range(2):
+                nc.sync.dma_start(out=w3_raw[c][:, b], in_=group_rows(w3[:, N // 2 * c : N // 2 * (c + 1)], b))
 
-        def weigh(signed_h, bank, slope_part):
-            nc.vector.tensor_tensor(out=signed_h, in0=bank[:], in1=slope_part, op=ALU.mult)
+        def weave_w3(c):
+            w3_woven[c] = work([P, 2, N // 2, PACK], BF16, "w3_woven%d" % c)
+            nc.scalar.activation(out=w3_woven[c][:], in_=w3_raw[c][:].rearrange("p b t n -> p b n t"), func=ACT.Copy)
 
-        def interleave_h(b, hf, signed_h):
-            h_woven[b, hf] = shared([P, HALF, PACK], BF16, "h_woven%d_%d" % (b, hf), "woven_h", 2)
-            nc.scalar.activation(out=h_woven[b, hf][:], in_=signed_h[:].rearrange("p t j -> p j t"), func=ACT.Abs)
+        def quantise_w3(c):
+            w3_mx[c] = quantise(w3_woven[c][:].rearrange("p b n t -> p (b n t)"), "w3_%d" % c)
 
-        def quantise_h(b, hf, tag, bufs):
-            h_mx[b, hf] = quantise(h_woven[b, hf], "h%d_%d" % (b, hf), tag, bufs)
+        def weigh(b, hf, t):
+            if t == 0:
+                signed_h[b, hf] = work([P, PACK, HALF], BF16, "signed_h%d_%d" % (b, hf))
+            bank = psum.tile([P, HALF], F32, name="d%d_%d_%d" % (b, hf, t), tag="bank%d_%d" % (hf, t))
+            cols = slice(P * t, P * (t + 1))
+            cols_of_all = slice(PASS * b + P * t, PASS * b + P * (t + 1))
+            passes = [(wa_mx[b, a][0][:, cols], wa_mx[b, a][1][:, cols], a) for a in range(2)]
+            passes = passes + [(wb_codes[a][:, cols_of_all], wb_ordered_plane[:, a, cols_of_all], a) for a in range(2)]
+            for number, (codes, plane, a) in enumerate(passes):
+                nc.tensor.matmul_mx(
+                    out=bank[:],
+                    lhsT=codes.bitcast(E4M3),
+                    lhsT_scale=plane,
+                    rhs=v_words[a][:, half_cols(hf)].bitcast(E5M2),
+                    rhs_scale=v_planes[a][:, half_cols(hf)],
+                    start=(number == 0),
+                    stop=(number == len(passes) - 1),
+                )
+            nc.vector.tensor_tensor(out=signed_h[b, hf][:, t, :], in0=bank[:], in1=slopes[b, t, hf], op=ALU.mult)
 
-        pick(0, 0)
+        def weave_h(b, hf):
+            h_woven[b, hf] = work([P, HALF, PACK], BF16, "h_woven%d_%d" % (b, hf))
+            nc.scalar.activation(out=h_woven[b, hf][:], in_=signed_h[b, hf][:].rearrange("p t j -> p j t"), func=ACT.Abs)
+
+        def quantise_h(b, hf):
+            h_mx[b, hf] = quantise(h_woven[b, hf][:].rearrange("p j t -> p (j t)"), "h%d_%d" % (b, hf))
+
+        def audit(hf, n):
+            bank = psum.tile([P, HALF], F32, name="y%d_%d" % (hf, n), tag="bank%d_%d" % (hf, n))
+            for b in range(2):
+                cols = slice(N // 2 * b + P * (n % 2), N // 2 * b + P * (n % 2 + 1))
+                nc.tensor.matmul_mx(
+                    out=bank[:],
+                    lhsT=w3_mx[n // 2][0][:, cols].bitcast(E4M3),
+                    lhsT_scale=w3_mx[n // 2][1][:, cols],
+                    rhs=h_mx[b, hf][0][:].bitcast(E4M3),
+                    rhs_scale=h_mx[b, hf][1][:],
+                    start=(b == 0),
+                    stop=(b == 1),
+                )
+            y = work([P, HALF], F32, "y_sb%d_%d" % (hf, n))
+            nc.scalar.copy(out=y[:], in_=bank[:])
+            nc.vector.tensor_tensor(pages[n][:].indirect(half_list(idx2, hf)), y[:], gains[:, half_cols(hf)], ALU.mult)
+            if hf == 1:
+                nc.sync.dma_start(out=out[P * n : P * (n + 1), :], in_=pages[n][:])
+
+        both = (0, 1)
+        load_s(0, 0)
+        pick(0, 0, both)
         load_wb_scale_rows(0)
-        pick(0, 1)
-        slope(0, 0)
-        slope(0, 1)
+        weave_wa(0, 0)
         load_wb_scale_rows(1)
-        quantise_wa(0, 0)
         load_wb_scale_rows(2)
-        pick(0, 2)
-        quantise_wa(0, 1)
         load_wb_scale_rows(3)
-        order_wb(0)
-        wb_ordered_plane = held([P, 2, H], U8, "wb_ordered_plane")
-        nc.vector.tensor_copy(
-            out=wb_ordered_plane[:].rearrange("p a (b t m) -> p (a b) t m", b=2, t=PACK),
-            in_=wb_plane[:].rearrange("p a (b m t) -> p (a b) t m", b=2, t=PACK),
-        )
-        pick(0, 3)
-        slope(0, 2)
-        slope(0, 3)
-        quantise_wa(1, 0)
-        quantise_wa(1, 1)
-        order_wb(1)
+        wb_ordered_plane = order_wb_plane()
+        slope(0, 0, both, True)
+        weave_wa(0, 1)
+        quantise_wa(0, 0)
+        wb_raw = load_wb()
+        order_wb(wb_raw, 0)
+        order_wb(wb_raw, 1)
+        quantise_wa(0, 1)
+        load_s(0, 1)
+        pick(0, 1, both)
         for hf in range(2):
-            banks = differences(0, hf)
-            signed_h = held([P, PACK, HALF], F32, "signed_h0_%d" % hf)
-            for t in range(PACK):
-                weigh(signed_h[:, t, :], banks[t], slopes[0, t][:, half_cols(hf)])
-            interleave_h(0, hf, signed_h)
-
-        pick(1, 0)
-        pick(1, 1)
-        slope(1, 0)
-        slope(1, 1)
-        interleave_w3(0)
-        interleave_w3(1)
+            weigh(0, hf, 0)
+        slope(0, 1, both, True)
+        weave_wa(1, 0)
+        for hf in range(2):
+            weigh(0, hf, 1)
+        quantise_wa(1, 0)
+        weave_wa(1, 1)
+        load_s(0, 2)
+        pick(0, 2, both)
+        quantise_wa(1, 1)
+        load_s(0, 3)
+        pick(0, 3, both)
+        slope(0, 2, both, False)
+        for hf in range(2):
+            weigh(0, hf, 2)
+        load_s(1, 0)
+        pick(1, 0, both)
+        slope(0, 3, both, False)
+        for hf in range(2):
+            weigh(0, hf, 3)
+        load_s(1, 1)
+        pick(1, 1, both)
+        slope(1, 0, both, False)
         load_s(1, 2)
+        pick(1, 2, (0,))
+        slope(1, 1, both, False)
+        weave_h(0, 0)
         load_s(1, 3)
+        pick(1, 3, (0,))
+        weigh(1, 0, 0)
+        slope(1, 2, (0,), False)
+        pick(1, 2, (1,))
+        slope(1, 3, (0,), False)
+        pick(1, 3, (1,))
+        load_w3(0)
+        weave_w3(0)
         idx2 = lists.tile([P, LIST_COLS], U16, name="idx2")
         nc.sync.dma_start(idx2[:], offs2)
         gains = stream([P, S], F32, "gains")
         nc.sync.dma_start(out=gains[:], in_=wgo)
-
-        for hf in range(2):
-            banks = differences(1, hf)
-            late_slopes = shared([P, 2, HALF], F32, "late_slopes%d" % hf, "after_slopes", AFTER_BUFS)
-            signed_h = shared([P, PACK, HALF], F32, "signed_h1_%d" % hf, "late", 1)
-            for t in range(2):
-                weigh(signed_h[:, t, :], banks[t], slopes[1, t][:, half_cols(hf)])
-            for t in range(2, PACK):
-                part = late_slopes[:, t - 2, :]
-                nc.vector.tensor_copy(part, s_rows[1, t][:].indirect(half_list(idx, hf)))
-                minus_slope(part, part)
-                weigh(signed_h[:, t, :], banks[t], part)
-            if hf == 0:
-                quantise_h(0, 0, "after_slopes", AFTER_BUFS)
-                for b in range(2):
-                    w3_mx[b] = quantise(w3_woven[b], "w3_%d" % b, "after_slopes", AFTER_BUFS)
-            interleave_h(1, hf, signed_h)
-            quantise_h(1, hf, "h_codes", 3)
-            if hf == 0:
-                quantise_h(0, 1, "h_codes", 3)
-
-        for hf in range(2):
-            for n in range(N // P):
-                bank = psum.tile([P, HALF], F32, name="y%d_%d" % (hf, n), tag="bank")
-                cols = slice(P * n, P * (n + 1))
-                for b in range(2):
-                    nc.tensor.matmul_mx(
-                        out=bank[:],
-                        lhsT=w3_mx[b][0][:, cols].bitcast(E4M3),
-                        lhsT_scale=w3_mx[b][1][:, cols],
-                        rhs=h_mx[b, hf][0][:].bitcast(E4M3),
-                        rhs_scale=h_mx[b, hf][1][:],
-                        start=(b == 0),
-                        stop=(b == 1),
-                    )
-                if hf == 0 and n == N // P - 1:
-                    y = shared([P, HALF], F32, "y_late", "late", 1)
-                else:
-                    y = shared([P, HALF], F32, "y_sb%d_%d" % (hf, n), "y", Y_BUFS)
-                nc.scalar.copy(out=y[:], in_=bank[:])
-                nc.vector.tensor_tensor(pages[n][:].indirect(half_list(idx2, hf)), y[:], gains[:, half_cols(hf)], ALU.mult)
-                if hf == 1:
-                    nc.sync.dma_start(out=out[cols, :], in_=pages[n][:])
+        load_w3(1)
+        for t in range(1, PACK):
+            weigh(1, 0, t)
+        weave_h(1, 0)
+        weigh(1, 1, 0)
+        weigh(1, 1, 1)
+        quantise_h(0, 0)
+        quantise_w3(0)
+        quantise_h(1, 0)
+        slope(1, 2, (1,), True)
+        slope(1, 3, (1,), True)
+        weigh(1, 1, 2)
+        weigh(1, 1, 3)
+        audit(0, 0)
+        weave_w3(1)
+        quantise_w3(1)
+        audit(0, 1)
+        weave_h(0, 1)
+        quantise_h(0, 1)
+        audit(0, 2)
+        weave_h(1, 1)
+        quantise_h(1, 1)
+        audit(0, 3)
+        for n in range(N // P):
+            audit(1, n)

@@ -22,7 +22,7 @@ PASS = P * PACK
 HALF = 512
 QUADRANTS = 4
 LIST_COLS = S // 16
-STREAM_BUFS = 9
+STREAM_BUFS = 10
 WORK_BUFS = 30
 
 
@@ -59,15 +59,15 @@ def tile_list_advisor_disagreement_audit_kernel(
             nc.vector.quantize_mx(out=codes[:].bitcast(E4M3), scales=plane[:], in_=woven)
             return codes, plane
 
-        tab_plane = held([P, T], U8, "tab_plane")
+        tab_plane = keep.tile([P, T], U8, name="tab_plane", tag="plane_then_page", bufs=1, align_bytes=64)
         wb_plane = stream([P, 2, H], U8, "wb_plane")
         v_planes = [work([P, S], U8, "v_plane0"), held([P, S], U8, "v_plane1")]
-        nc.gpsimd.memset(tab_plane[:].bitcast(I32), 0)
-        nc.gpsimd.memset(v_planes[1][:].bitcast(I32), 0)
-        nc.gpsimd.memset(wb_plane[:].bitcast(I32), 0)
-        pages = [held([P, T2], F32, "page%d" % n) for n in range(N // P)]
-        for page in pages:
-            nc.gpsimd.memset(page[:], 0.0)
+        pages = [held([P, T2], F32, "page%d" % n) for n in range(2)]
+        nc.vector.memset(tab_plane[:].bitcast(I32), 0)
+        nc.vector.memset(pages[0][:], 0.0)
+        nc.vector.memset(wb_plane[:].bitcast(I32), 0)
+        nc.vector.memset(v_planes[1][:].bitcast(I32), 0)
+        nc.vector.memset(pages[1][:], 0.0)
 
         idx = lists.tile([P, LIST_COLS], U16, name="idx")
         nc.sync.dma_start(idx[:], offs)
@@ -80,7 +80,9 @@ def tile_list_advisor_disagreement_audit_kernel(
             nc.sync.dma_start(out=tab[a][:], in_=tab_words[a].rearrange("p t i -> p (t i)").bitcast(I32))
         nc.vector.tensor_copy(v_planes[0][:], tab_plane[:].indirect(idx[:]))
         live = 32 * (QUADRANTS - 1) + 4
-        nc.sync.dma_start(out=v_planes[1][0:live, :].bitcast(I32), in_=v_planes[0][4 : live + 4, :].bitcast(I32))
+        nc.scalar.dma_start(out=v_planes[1][0:live, :].bitcast(I32), in_=v_planes[0][4 : live + 4, :].bitcast(I32))
+        pages.append(keep.tile([P, T2], F32, name="page2", tag="plane_then_page", bufs=1, align_bytes=64))
+        nc.gpsimd.memset(pages[2][:], 0.0)
         v_words = [work([P, S], U32, "v_words%d" % a) for a in range(2)]
         for a in range(2):
             nc.vector.tensor_copy(v_words[a][:], tab[a][:].bitcast(U32).indirect(idx[:]))
@@ -220,6 +222,8 @@ def tile_list_advisor_disagreement_audit_kernel(
         weave_wa(0, 1)
         quantise_wa(0, 0)
         wb_raw = load_wb()
+        pages.append(stream([P, T2], F32, "page3"))
+        nc.gpsimd.memset(pages[3][:], 0.0)
         order_wb(wb_raw, 0)
         order_wb(wb_raw, 1)
         quantise_wa(0, 1)

@@ -116,8 +116,8 @@ def tile_list_advisor_disagreement_audit_kernel(
             nc.sync.dma_start(out=raw[:], in_=group_rows(wa[:, PASS * b : PASS * (b + 1)], a))
             wa_woven[b, a] = work([P, PASS, PACK], BF16, "wa_woven%d_%d" % (b, a))
             nc.scalar.activation(
-                out=wa_woven[b, a][:].rearrange("p (t m) i -> p m t i", t=PACK),
-                in_=raw[:].rearrange("p i (m t) -> p m t i", t=PACK),
+                out=wa_woven[b, a][:].rearrange("p (t m) i -> p m i t", t=PACK),
+                in_=raw[:].rearrange("p i (m t) -> p m i t", t=PACK),
                 func=ACT.Copy,
                 scale=-1.0,
             )
@@ -158,7 +158,10 @@ def tile_list_advisor_disagreement_audit_kernel(
 
         def weave_w3(c):
             w3_woven[c] = work([P, 2, N // 2, PACK], BF16, "w3_woven%d" % c)
-            nc.scalar.activation(out=w3_woven[c][:], in_=w3_raw[c][:].rearrange("p b t n -> p b n t"), func=ACT.Copy)
+            nc.scalar.copy(
+                out=w3_woven[c][:].rearrange("p b (g e) t -> p b g t e", e=4),
+                in_=w3_raw[c][:].rearrange("p b t (g e) -> p b g t e", e=4),
+            )
 
         def quantise_w3(c):
             w3_mx[c] = quantise(w3_woven[c][:].rearrange("p b n t -> p (b n t)"), "w3_%d" % c)
@@ -185,7 +188,11 @@ def tile_list_advisor_disagreement_audit_kernel(
 
         def weave_h(b, hf):
             h_woven[b, hf] = work([P, HALF, PACK], BF16, "h_woven%d_%d" % (b, hf))
-            nc.scalar.activation(out=h_woven[b, hf][:], in_=signed_h[b, hf][:].rearrange("p t j -> p j t"), func=ACT.Abs)
+            nc.scalar.activation(
+                out=h_woven[b, hf][:].rearrange("p (g e) t -> p g t e", e=4),
+                in_=signed_h[b, hf][:].rearrange("p t (g e) -> p g t e", e=4),
+                func=ACT.Abs,
+            )
 
         def quantise_h(b, hf):
             h_mx[b, hf] = quantise(h_woven[b, hf][:].rearrange("p j t -> p (j t)"), "h%d_%d" % (b, hf))

@@ -23,7 +23,7 @@ HALF = 512
 QUADRANTS = 4
 LIST_COLS = S // 16
 STREAM_BUFS = 10
-WORK_BUFS = 30
+WORK_BUFS = 32
 
 
 def tile_list_advisor_disagreement_audit_kernel(
@@ -87,8 +87,9 @@ def tile_list_advisor_disagreement_audit_kernel(
         for a in range(2):
             nc.vector.tensor_copy(v_words[a][:], tab[a][:].bitcast(U32).indirect(idx[:]))
 
+        rests = {}
         s_rows, picked, slopes, wa_woven, wa_mx, wb_codes, signed_h = {}, {}, {}, {}, {}, {}, {}
-        w3_raw, w3_woven, w3_mx, h_woven, h_mx = {}, {}, {}, {}, {}
+        wb_raw, w3_raw, w3_woven, w3_mx, h_woven, h_mx = {}, {}, {}, {}, {}, {}
 
         def load_s(b, t):
             s_rows[b, t] = stream([P, T], F32, "s_rows%d_%d" % (b, t))
@@ -100,14 +101,19 @@ def tile_list_advisor_disagreement_audit_kernel(
             entries = idx[:] if len(halves) == 2 else half_list(idx, halves[0])
             nc.vector.tensor_copy(picked[b, t, halves][:], s_rows[b, t][:].indirect(entries))
 
+        def rest(b, t, halves):
+            rests[b, t, halves] = work([P, HALF * len(halves)], F32, "rest%d_%d_%d" % (b, t, halves[0]))
+            nc.scalar.activation(
+                out=rests[b, t, halves][:], in_=picked[b, t, halves][:], func=ACT.Copy, scale=-1.0, bias=1.0
+            )
+
         def slope(b, t, halves, on_vector):
             s = picked[b, t, halves][:]
             made = work([P, HALF * len(halves)], F32, "slope%d_%d_%d" % (b, t, halves[0]))
             if on_vector:
                 nc.vector.scalar_tensor_tensor(out=made[:], in0=s, scalar=1.0, in1=s, op0=ALU.subtract, op1=ALU.mult)
             else:
-                nc.scalar.activation(out=made[:], in_=s, func=ACT.Copy, scale=-1.0, bias=1.0)
-                nc.gpsimd.tensor_tensor(out=made[:], in0=made[:], in1=s, op=ALU.mult)
+                nc.gpsimd.tensor_tensor(out=made[:], in0=rests[b, t, halves][:], in1=s, op=ALU.mult)
             for place, hf in enumerate(halves):
                 slopes[b, t, hf] = made[:, half_cols(place)]
 
@@ -131,16 +137,16 @@ def tile_list_advisor_disagreement_audit_kernel(
                 in_=wb_scales[:, 4 * q : 4 * q + 4, :].rearrange("a r c -> r a c").bitcast(I32),
             )
 
-        def load_wb():
-            raw = stream([P, 2, H], I32, "wb_raw")
-            nc.sync.dma_start(out=raw[:], in_=wb_words.rearrange("a p c i -> p a (c i)").bitcast(I32))
-            return raw
+        def load_wb(b):
+            wb_raw[b] = stream([P, 2, PASS], I32, "wb_raw%d" % b)
+            words = wb_words[:, :, PASS * b : PASS * (b + 1), :].rearrange("a p c i -> p a (c i)")
+            nc.sync.dma_start(out=wb_raw[b][:], in_=words.bitcast(I32))
 
-        def order_wb(raw, a):
-            wb_codes[a] = work([P, H], I32, "wb_codes%d" % a)
-            nc.vector.tensor_copy(
-                out=wb_codes[a][:].rearrange("p (b t g e) -> p b g t e", b=2, t=PACK, e=4),
-                in_=raw[:, a, :].rearrange("p (b g e t) -> p b g t e", b=2, t=PACK, e=4),
+        def order_wb(b):
+            wb_codes[b] = work([P, 2, PASS], I32, "wb_codes%d" % b)
+            (nc.vector, nc.gpsimd)[b].tensor_copy(
+                out=wb_codes[b][:].rearrange("p a (t g e) -> p a g t e", t=PACK, e=4),
+                in_=wb_raw[b][:].rearrange("p a (g e t) -> p a g t e", t=PACK, e=4),
             )
 
         def order_wb_plane():
@@ -172,8 +178,14 @@ def tile_list_advisor_disagreement_audit_kernel(
             bank = psum.tile([P, HALF], F32, name="d%d_%d_%d" % (b, hf, t), tag="bank%d_%d" % (hf, t))
             cols = slice(P * t, P * (t + 1))
             cols_of_all = slice(PASS * b + P * t, PASS * b + P * (t + 1))
-            passes = [(wa_mx[b, a][0][:, cols], wa_mx[b, a][1][:, cols], a) for a in range(2)]
-            passes = passes + [(wb_codes[a][:, cols_of_all], wb_ordered_plane[:, a, cols_of_all], a) for a in range(2)]
+            passes = [(wb_codes[b][:, a, cols], wb_ordered_plane[:, a, cols_of_all], a) for a in range(2)]
+            wa_passes = [(wa_mx[b, a][0][:, cols], wa_mx[b, a][1][:, cols], a) for a in range(2)]
+            if b == 0:
+                passes = wa_passes[:1] + passes + wa_passes[1:]
+            elif t < PACK - 1:
+                passes = passes + wa_passes
+            else:
+                passes = wa_passes[::-1] + passes
             for number, (codes, plane, a) in enumerate(passes):
                 nc.tensor.matmul_mx(
                     out=bank[:],
@@ -220,73 +232,83 @@ def tile_list_advisor_disagreement_audit_kernel(
         load_s(0, 0)
         pick(0, 0, both)
         load_wb_scale_rows(0)
-        weave_wa(0, 0)
         load_wb_scale_rows(1)
+        rest(0, 0, both)
+        slope(0, 0, both, False)
+        weave_wa(0, 0)
         load_wb_scale_rows(2)
         load_wb_scale_rows(3)
         wb_ordered_plane = order_wb_plane()
-        slope(0, 0, both, True)
-        weave_wa(0, 1)
-        quantise_wa(0, 0)
-        wb_raw = load_wb()
+        load_s(0, 1)
         pages.append(stream([P, T2], F32, "page3"))
         nc.gpsimd.memset(pages[3][:], 0.0)
-        order_wb(wb_raw, 0)
-        order_wb(wb_raw, 1)
-        quantise_wa(0, 1)
-        load_s(0, 1)
         pick(0, 1, both)
-        for hf in range(2):
-            weigh(0, hf, 0)
+        quantise_wa(0, 0)
+        weave_wa(0, 1)
         slope(0, 1, both, True)
-        weave_wa(1, 0)
-        for hf in range(2):
-            weigh(0, hf, 1)
-        quantise_wa(1, 0)
-        weave_wa(1, 1)
+        load_wb(0)
+        order_wb(0)
+        quantise_wa(0, 1)
         load_s(0, 2)
         pick(0, 2, both)
-        quantise_wa(1, 1)
+        load_wb(1)
+        order_wb(1)
+        rest(0, 2, both)
+        for hf in range(2):
+            weigh(0, hf, 0)
         load_s(0, 3)
         pick(0, 3, both)
-        slope(0, 2, both, False)
+        rest(0, 3, both)
         for hf in range(2):
-            weigh(0, hf, 2)
+            weigh(0, hf, 1)
         load_s(1, 0)
         pick(1, 0, both)
+        slope(0, 2, both, False)
+        weave_wa(1, 0)
+        quantise_wa(1, 0)
+        rest(1, 0, both)
+        for hf in range(2):
+            weigh(0, hf, 2)
+        load_s(1, 1)
+        pick(1, 1, both)
         slope(0, 3, both, False)
         for hf in range(2):
             weigh(0, hf, 3)
-        load_s(1, 1)
-        pick(1, 1, both)
-        slope(1, 0, both, False)
+        weave_wa(1, 1)
+        rest(1, 1, both)
+        quantise_wa(1, 1)
+        weave_h(0, 0)
         load_s(1, 2)
         pick(1, 2, (0,))
-        slope(1, 1, both, False)
-        weave_h(0, 0)
+        slope(1, 0, both, False)
+        rest(1, 2, (0,))
+        weigh(1, 0, 0)
         load_s(1, 3)
         pick(1, 3, (0,))
-        weigh(1, 0, 0)
-        slope(1, 2, (0,), False)
+        slope(1, 1, both, False)
+        rest(1, 3, (0,))
+        weigh(1, 0, 1)
         pick(1, 2, (1,))
+        slope(1, 2, (0,), False)
         slope(1, 3, (0,), False)
-        pick(1, 3, (1,))
         load_w3(0)
         weave_w3(0)
+        rest(1, 2, (1,))
+        slope(1, 2, (1,), False)
         idx2 = lists.tile([P, LIST_COLS], U16, name="idx2")
         nc.sync.dma_start(idx2[:], offs2)
         gains = stream([P, S], F32, "gains")
         nc.sync.dma_start(out=gains[:], in_=wgo)
         load_w3(1)
-        for t in range(1, PACK):
+        for t in range(2, PACK):
             weigh(1, 0, t)
         weave_h(1, 0)
+        pick(1, 3, (1,))
         weigh(1, 1, 0)
         weigh(1, 1, 1)
         quantise_h(0, 0)
         quantise_w3(0)
         quantise_h(1, 0)
-        slope(1, 2, (1,), True)
         slope(1, 3, (1,), True)
         weigh(1, 1, 2)
         weigh(1, 1, 3)

@@ -55,7 +55,10 @@ def tile_list_advisor_disagreement_audit_kernel(
 
         def quantise(woven, name):
             codes = work([P, PASS], U32, name + "_codes")
-            plane = held([P, PASS], U8, name + "_plane")
+            if name == "wa1_0":
+                plane = lists.tile([P, PASS], U8, name=name + "_plane", tag="late_list", bufs=2, align_bytes=64)
+            else:
+                plane = held([P, PASS], U8, name + "_plane")
             nc.vector.quantize_mx(out=codes[:].bitcast(E4M3), scales=plane[:], in_=woven)
             return codes, plane
 
@@ -71,7 +74,7 @@ def tile_list_advisor_disagreement_audit_kernel(
 
         idx = lists.tile([P, LIST_COLS], U16, name="idx")
         nc.sync.dma_start(idx[:], offs)
-        for q in range(QUADRANTS):
+        for q in (0, 2, 1, 3):
             nc.sync.dma_start(
                 out=tab_plane[32 * q : 32 * q + 8, :].bitcast(I32), in_=tab_scales[:, 4 * q : 4 * q + 4, :].bitcast(I32)
             )
@@ -81,6 +84,11 @@ def tile_list_advisor_disagreement_audit_kernel(
         nc.vector.tensor_copy(v_planes[0][:], tab_plane[:].indirect(idx[:]))
         live = 32 * (QUADRANTS - 1) + 4
         nc.scalar.dma_start(out=v_planes[1][0:live, :].bitcast(I32), in_=v_planes[0][4 : live + 4, :].bitcast(I32))
+        for q in (0, 2, 1, 3):
+            nc.gpsimd.dma_start(
+                out=wb_plane[32 * q : 32 * q + 4, :, :].bitcast(I32),
+                in_=wb_scales[:, 4 * q : 4 * q + 4, :].rearrange("a r c -> r a c").bitcast(I32),
+            )
         pages.append(keep.tile([P, T2], F32, name="page2", tag="plane_then_page", bufs=1, align_bytes=64))
         nc.gpsimd.memset(pages[2][:], 0.0)
         v_words = [work([P, S], U32, "v_words%d" % a) for a in range(2)]
@@ -130,12 +138,6 @@ def tile_list_advisor_disagreement_audit_kernel(
 
         def quantise_wa(b, a):
             wa_mx[b, a] = quantise(wa_woven[b, a][:].rearrange("p c i -> p (c i)"), "wa%d_%d" % (b, a))
-
-        def load_wb_scale_rows(q):
-            nc.sync.dma_start(
-                out=wb_plane[32 * q : 32 * q + 4, :, :].bitcast(I32),
-                in_=wb_scales[:, 4 * q : 4 * q + 4, :].rearrange("a r c -> r a c").bitcast(I32),
-            )
 
         def load_wb(b):
             wb_raw[b] = stream([P, 2, PASS], I32, "wb_raw%d" % b)
@@ -231,13 +233,9 @@ def tile_list_advisor_disagreement_audit_kernel(
         both = (0, 1)
         load_s(0, 0)
         pick(0, 0, both)
-        load_wb_scale_rows(0)
-        load_wb_scale_rows(1)
         rest(0, 0, both)
         slope(0, 0, both, False)
         weave_wa(0, 0)
-        load_wb_scale_rows(2)
-        load_wb_scale_rows(3)
         wb_ordered_plane = order_wb_plane()
         load_s(0, 1)
         pages.append(stream([P, T2], F32, "page3"))
@@ -295,7 +293,7 @@ def tile_list_advisor_disagreement_audit_kernel(
         weave_w3(0)
         rest(1, 2, (1,))
         slope(1, 2, (1,), False)
-        idx2 = lists.tile([P, LIST_COLS], U16, name="idx2")
+        idx2 = lists.tile([P, LIST_COLS], U16, name="idx2", tag="late_list", bufs=2, align_bytes=64)
         nc.sync.dma_start(idx2[:], offs2)
         gains = stream([P, S], F32, "gains")
         nc.sync.dma_start(out=gains[:], in_=wgo)

@@ -22,7 +22,7 @@ PASS = P * PACK
 HALF = 512
 QUADRANTS = 4
 LIST_COLS = S // 16
-STREAM_BUFS = 10
+STREAM_BUFS = 9
 WORK_BUFS = 32
 
 
@@ -63,14 +63,19 @@ def tile_list_advisor_disagreement_audit_kernel(
             return codes, plane
 
         tab_plane = keep.tile([P, T], U8, name="tab_plane", tag="plane_then_page", bufs=1, align_bytes=64)
+        tab = [stream([P, T], I32, "tab0")]
         wb_plane = stream([P, 2, H], U8, "wb_plane")
+        tab.append(stream([P, T], I32, "tab1"))
+        v_words = [work([P, S], U32, "v_words0")]
         v_planes = [work([P, S], U8, "v_plane0"), held([P, S], U8, "v_plane1")]
-        pages = [held([P, T2], F32, "page%d" % n) for n in range(2)]
+        v_words.append(work([P, S], U32, "v_words1"))
+        pages = [held([P, T2], F32, "page%d" % n) for n in range(3)]
         nc.vector.memset(tab_plane[:].bitcast(I32), 0)
         nc.vector.memset(pages[0][:], 0.0)
         nc.vector.memset(wb_plane[:].bitcast(I32), 0)
         nc.vector.memset(v_planes[1][:].bitcast(I32), 0)
-        nc.vector.memset(pages[1][:], 0.0)
+        for page in pages[1:]:
+            nc.vector.memset(page[:], 0.0)
 
         idx = lists.tile([P, LIST_COLS], U16, name="idx")
         nc.sync.dma_start(idx[:], offs)
@@ -78,7 +83,6 @@ def tile_list_advisor_disagreement_audit_kernel(
             nc.sync.dma_start(
                 out=tab_plane[32 * q : 32 * q + 8, :].bitcast(I32), in_=tab_scales[:, 4 * q : 4 * q + 4, :].bitcast(I32)
             )
-        tab = [stream([P, T], I32, "tab%d" % a) for a in range(2)]
         for a in range(2):
             nc.sync.dma_start(out=tab[a][:], in_=tab_words[a].rearrange("p t i -> p (t i)").bitcast(I32))
         nc.vector.tensor_copy(v_planes[0][:], tab_plane[:].indirect(idx[:]))
@@ -89,9 +93,8 @@ def tile_list_advisor_disagreement_audit_kernel(
                 out=wb_plane[32 * q : 32 * q + 4, :, :].bitcast(I32),
                 in_=wb_scales[:, 4 * q : 4 * q + 4, :].rearrange("a r c -> r a c").bitcast(I32),
             )
-        pages.append(keep.tile([P, T2], F32, name="page2", tag="plane_then_page", bufs=1, align_bytes=64))
-        nc.gpsimd.memset(pages[2][:], 0.0)
-        v_words = [work([P, S], U32, "v_words%d" % a) for a in range(2)]
+        pages.append(keep.tile([P, T2], F32, name="page3", tag="plane_then_page", bufs=1, align_bytes=64))
+        nc.gpsimd.memset(pages[3][:], 0.0)
         for a in range(2):
             nc.vector.tensor_copy(v_words[a][:], tab[a][:].bitcast(U32).indirect(idx[:]))
 
@@ -109,10 +112,30 @@ def tile_list_advisor_disagreement_audit_kernel(
             entries = idx[:] if len(halves) == 2 else half_list(idx, halves[0])
             nc.vector.tensor_copy(picked[b, t, halves][:], s_rows[b, t][:].indirect(entries))
 
-        def rest(b, t, halves):
-            rests[b, t, halves] = work([P, HALF * len(halves)], F32, "rest%d_%d_%d" % (b, t, halves[0]))
+        def rest(b, t, halves, over=None):
+            if over is None:
+                rests[b, t, halves] = work([P, HALF * len(halves)], F32, "rest%d_%d_%d" % (b, t, halves[0]))[:]
+            else:
+                rests[b, t, halves] = over[:].rearrange("p c i -> p (c i)").bitcast(F32)
             nc.scalar.activation(
-                out=rests[b, t, halves][:], in_=picked[b, t, halves][:], func=ACT.Copy, scale=-1.0, bias=1.0
+                out=rests[b, t, halves], in_=picked[b, t, halves][:], func=ACT.Copy, scale=-1.0, bias=1.0
+            )
+
+        def slope_half(b, t, hf):
+            made = work([P, HALF], F32, "slope%d_%d_%d" % (b, t, hf))
+            nc.gpsimd.tensor_tensor(
+                out=made[:], in0=rests[b, t, both][:, half_cols(hf)], in1=picked[b, t, both][:, half_cols(hf)], op=ALU.mult
+            )
+            slopes[b, t, hf] = made[:]
+
+        def weave_h_part(b, hf, part):
+            if part == 0:
+                h_woven[b, hf] = work([P, HALF, PACK], BF16, "h_woven%d_%d" % (b, hf))
+            cols = slice(HALF // 2 * part, HALF // 2 * (part + 1))
+            nc.scalar.activation(
+                out=h_woven[b, hf][:, cols, :].rearrange("p (g e) t -> p g t e", e=4),
+                in_=signed_h[b, hf][:, :, cols].rearrange("p t (g e) -> p g t e", e=4),
+                func=ACT.Abs,
             )
 
         def slope(b, t, halves, on_vector):
@@ -121,7 +144,7 @@ def tile_list_advisor_disagreement_audit_kernel(
             if on_vector:
                 nc.vector.scalar_tensor_tensor(out=made[:], in0=s, scalar=1.0, in1=s, op0=ALU.subtract, op1=ALU.mult)
             else:
-                nc.gpsimd.tensor_tensor(out=made[:], in0=rests[b, t, halves][:], in1=s, op=ALU.mult)
+                nc.gpsimd.tensor_tensor(out=made[:], in0=rests[b, t, halves], in1=s, op=ALU.mult)
             for place, hf in enumerate(halves):
                 slopes[b, t, hf] = made[:, half_cols(place)]
 
@@ -233,20 +256,18 @@ def tile_list_advisor_disagreement_audit_kernel(
         both = (0, 1)
         load_s(0, 0)
         pick(0, 0, both)
-        rest(0, 0, both)
-        slope(0, 0, both, False)
         weave_wa(0, 0)
-        wb_ordered_plane = order_wb_plane()
-        load_s(0, 1)
-        pages.append(stream([P, T2], F32, "page3"))
-        nc.gpsimd.memset(pages[3][:], 0.0)
-        pick(0, 1, both)
         quantise_wa(0, 0)
+        rest(0, 0, both)
+        wb_ordered_plane = order_wb_plane()
+        slope(0, 0, both, False)
+        load_s(0, 1)
+        pick(0, 1, both)
         weave_wa(0, 1)
-        slope(0, 1, both, True)
         load_wb(0)
         order_wb(0)
         quantise_wa(0, 1)
+        rest(0, 1, both, wa_woven[0, 1])
         load_s(0, 2)
         pick(0, 2, both)
         load_wb(1)
@@ -256,6 +277,7 @@ def tile_list_advisor_disagreement_audit_kernel(
             weigh(0, hf, 0)
         load_s(0, 3)
         pick(0, 3, both)
+        slope(0, 1, both, False)
         rest(0, 3, both)
         for hf in range(2):
             weigh(0, hf, 1)
@@ -263,10 +285,10 @@ def tile_list_advisor_disagreement_audit_kernel(
         pick(1, 0, both)
         slope(0, 2, both, False)
         weave_wa(1, 0)
-        quantise_wa(1, 0)
-        rest(1, 0, both)
         for hf in range(2):
             weigh(0, hf, 2)
+        quantise_wa(1, 0)
+        rest(1, 0, both)
         load_s(1, 1)
         pick(1, 1, both)
         slope(0, 3, both, False)
@@ -275,7 +297,7 @@ def tile_list_advisor_disagreement_audit_kernel(
         weave_wa(1, 1)
         rest(1, 1, both)
         quantise_wa(1, 1)
-        weave_h(0, 0)
+        weave_h_part(0, 0, 0)
         load_s(1, 2)
         pick(1, 2, (0,))
         slope(1, 0, both, False)
@@ -283,12 +305,14 @@ def tile_list_advisor_disagreement_audit_kernel(
         weigh(1, 0, 0)
         load_s(1, 3)
         pick(1, 3, (0,))
-        slope(1, 1, both, False)
+        slope_half(1, 1, 0)
         rest(1, 3, (0,))
+        weave_h_part(0, 0, 1)
         weigh(1, 0, 1)
         pick(1, 2, (1,))
         slope(1, 2, (0,), False)
         slope(1, 3, (0,), False)
+        slope_half(1, 1, 1)
         load_w3(0)
         weave_w3(0)
         rest(1, 2, (1,))

@@ -23,7 +23,7 @@ HALF = 512
 QUADRANTS = 4
 LIST_COLS = S // 16
 STREAM_BUFS = 9
-WORK_BUFS = 32
+WORK_BUFS = 30
 
 
 def tile_list_advisor_disagreement_audit_kernel(
@@ -62,14 +62,14 @@ def tile_list_advisor_disagreement_audit_kernel(
             nc.vector.quantize_mx(out=codes[:].bitcast(E4M3), scales=plane[:], in_=woven)
             return codes, plane
 
-        tab_plane = keep.tile([P, T], U8, name="tab_plane", tag="plane_then_page", bufs=1, align_bytes=64)
+        tab_plane = held([P, T], U8, "tab_plane")
         tab = [stream([P, T], I32, "tab0")]
         wb_plane = stream([P, 2, H], U8, "wb_plane")
         tab.append(stream([P, T], I32, "tab1"))
         v_words = [work([P, S], U32, "v_words0")]
         v_planes = [work([P, S], U8, "v_plane0"), held([P, S], U8, "v_plane1")]
         v_words.append(work([P, S], U32, "v_words1"))
-        pages = [held([P, T2], F32, "page%d" % n) for n in range(3)]
+        pages = [held([P, T2], F32, "page%d" % n) for n in range(N // P)]
         nc.vector.memset(tab_plane[:].bitcast(I32), 0)
         nc.vector.memset(pages[0][:], 0.0)
         nc.vector.memset(wb_plane[:].bitcast(I32), 0)
@@ -93,8 +93,6 @@ def tile_list_advisor_disagreement_audit_kernel(
                 out=wb_plane[32 * q : 32 * q + 4, :, :].bitcast(I32),
                 in_=wb_scales[:, 4 * q : 4 * q + 4, :].rearrange("a r c -> r a c").bitcast(I32),
             )
-        pages.append(keep.tile([P, T2], F32, name="page3", tag="plane_then_page", bufs=1, align_bytes=64))
-        nc.gpsimd.memset(pages[3][:], 0.0)
         for a in range(2):
             nc.vector.tensor_copy(v_words[a][:], tab[a][:].bitcast(U32).indirect(idx[:]))
 
@@ -121,12 +119,15 @@ def tile_list_advisor_disagreement_audit_kernel(
                 out=rests[b, t, halves], in_=picked[b, t, halves][:], func=ACT.Copy, scale=-1.0, bias=1.0
             )
 
-        def slope_half(b, t, hf):
-            made = work([P, HALF], F32, "slope%d_%d_%d" % (b, t, hf))
+        def slope_half(b, t, hf, over=None):
+            if over is None:
+                made = work([P, HALF], F32, "slope%d_%d_%d" % (b, t, hf))[:]
+            else:
+                made = over[:].rearrange("p c i -> p (c i)").bitcast(F32)[:, 0:HALF]
             nc.gpsimd.tensor_tensor(
-                out=made[:], in0=rests[b, t, both][:, half_cols(hf)], in1=picked[b, t, both][:, half_cols(hf)], op=ALU.mult
+                out=made, in0=rests[b, t, both][:, half_cols(hf)], in1=picked[b, t, both][:, half_cols(hf)], op=ALU.mult
             )
-            slopes[b, t, hf] = made[:]
+            slopes[b, t, hf] = made
 
         def weave_h_part(b, hf, part):
             if part == 0:
@@ -175,8 +176,8 @@ def tile_list_advisor_disagreement_audit_kernel(
             )
 
         def order_wb_plane():
-            ordered = work([P, 2, H], U8, "wb_ordered_plane")
-            nc.vector.tensor_copy(
+            ordered = held([P, 2, H], U8, "wb_ordered_plane")
+            nc.gpsimd.tensor_copy(
                 out=ordered[:].rearrange("p a (b t m) -> p (a b) t m", b=2, t=PACK),
                 in_=wb_plane[:].rearrange("p a (b m t) -> p (a b) t m", b=2, t=PACK),
             )
@@ -205,9 +206,9 @@ def tile_list_advisor_disagreement_audit_kernel(
             cols_of_all = slice(PASS * b + P * t, PASS * b + P * (t + 1))
             passes = [(wb_codes[b][:, a, cols], wb_ordered_plane[:, a, cols_of_all], a) for a in range(2)]
             wa_passes = [(wa_mx[b, a][0][:, cols], wa_mx[b, a][1][:, cols], a) for a in range(2)]
-            if b == 0:
+            if (b, t) == (0, 0):
                 passes = wa_passes[:1] + passes + wa_passes[1:]
-            elif t < PACK - 1:
+            elif b == 1 and t < PACK - 1:
                 passes = passes + wa_passes
             else:
                 passes = wa_passes[::-1] + passes
@@ -256,13 +257,12 @@ def tile_list_advisor_disagreement_audit_kernel(
         both = (0, 1)
         load_s(0, 0)
         pick(0, 0, both)
-        weave_wa(0, 0)
-        quantise_wa(0, 0)
-        rest(0, 0, both)
         wb_ordered_plane = order_wb_plane()
-        slope(0, 0, both, False)
+        weave_wa(0, 0)
         load_s(0, 1)
         pick(0, 1, both)
+        quantise_wa(0, 0)
+        slope(0, 0, both, True)
         weave_wa(0, 1)
         load_wb(0)
         order_wb(0)
@@ -288,28 +288,29 @@ def tile_list_advisor_disagreement_audit_kernel(
         for hf in range(2):
             weigh(0, hf, 2)
         quantise_wa(1, 0)
-        rest(1, 0, both)
+        rest(1, 0, both, wa_woven[1, 0])
         load_s(1, 1)
         pick(1, 1, both)
         slope(0, 3, both, False)
+        slope_half(1, 0, 0)
         for hf in range(2):
             weigh(0, hf, 3)
         weave_wa(1, 1)
-        rest(1, 1, both)
         quantise_wa(1, 1)
         weave_h_part(0, 0, 0)
+        rest(1, 1, both)
         load_s(1, 2)
         pick(1, 2, (0,))
-        slope(1, 0, both, False)
+        slope_half(1, 0, 1, wa_woven[1, 1])
         rest(1, 2, (0,))
         weigh(1, 0, 0)
         load_s(1, 3)
         pick(1, 3, (0,))
-        slope_half(1, 1, 0)
-        rest(1, 3, (0,))
         weave_h_part(0, 0, 1)
-        weigh(1, 0, 1)
+        rest(1, 3, (0,))
         pick(1, 2, (1,))
+        slope_half(1, 1, 0)
+        weigh(1, 0, 1)
         slope(1, 2, (0,), False)
         slope(1, 3, (0,), False)
         slope_half(1, 1, 1)

@@ -23,7 +23,7 @@ HALF = 512
 QUADRANTS = 4
 LIST_COLS = S // 16
 STREAM_BUFS = 9
-WORK_BUFS = 30
+WORK_BUFS = 31
 
 
 def tile_list_advisor_disagreement_audit_kernel(
@@ -72,10 +72,10 @@ def tile_list_advisor_disagreement_audit_kernel(
         pages = [held([P, T2], F32, "page%d" % n) for n in range(N // P)]
         nc.vector.memset(tab_plane[:].bitcast(I32), 0)
         nc.vector.memset(pages[0][:], 0.0)
-        nc.vector.memset(wb_plane[:].bitcast(I32), 0)
         nc.vector.memset(v_planes[1][:].bitcast(I32), 0)
         for page in pages[1:]:
             nc.vector.memset(page[:], 0.0)
+        nc.vector.memset(wb_plane[:].bitcast(I32), 0)
 
         idx = lists.tile([P, LIST_COLS], U16, name="idx")
         nc.sync.dma_start(idx[:], offs)
@@ -176,7 +176,7 @@ def tile_list_advisor_disagreement_audit_kernel(
             )
 
         def order_wb_plane():
-            ordered = held([P, 2, H], U8, "wb_ordered_plane")
+            ordered = work([P, 2, H], U8, "wb_ordered_plane")
             nc.gpsimd.tensor_copy(
                 out=ordered[:].rearrange("p a (b t m) -> p (a b) t m", b=2, t=PACK),
                 in_=wb_plane[:].rearrange("p a (b m t) -> p (a b) t m", b=2, t=PACK),
@@ -208,7 +208,9 @@ def tile_list_advisor_disagreement_audit_kernel(
             wa_passes = [(wa_mx[b, a][0][:, cols], wa_mx[b, a][1][:, cols], a) for a in range(2)]
             if (b, t) == (0, 0):
                 passes = wa_passes[:1] + passes + wa_passes[1:]
-            elif b == 1 and t < PACK - 1:
+            elif b == 0:
+                passes = passes[::-1] + wa_passes[::-1]
+            elif t < PACK - 1:
                 passes = passes + wa_passes
             else:
                 passes = wa_passes[::-1] + passes
@@ -257,13 +259,13 @@ def tile_list_advisor_disagreement_audit_kernel(
         both = (0, 1)
         load_s(0, 0)
         pick(0, 0, both)
-        wb_ordered_plane = order_wb_plane()
         weave_wa(0, 0)
         load_s(0, 1)
         pick(0, 1, both)
         quantise_wa(0, 0)
         slope(0, 0, both, True)
         weave_wa(0, 1)
+        wb_ordered_plane = order_wb_plane()
         load_wb(0)
         order_wb(0)
         quantise_wa(0, 1)
@@ -313,6 +315,7 @@ def tile_list_advisor_disagreement_audit_kernel(
         weigh(1, 0, 1)
         slope(1, 2, (0,), False)
         slope(1, 3, (0,), False)
+        pick(1, 3, (1,))
         slope_half(1, 1, 1)
         load_w3(0)
         weave_w3(0)
@@ -326,7 +329,6 @@ def tile_list_advisor_disagreement_audit_kernel(
         for t in range(2, PACK):
             weigh(1, 0, t)
         weave_h(1, 0)
-        pick(1, 3, (1,))
         weigh(1, 1, 0)
         weigh(1, 1, 1)
         quantise_h(0, 0)

@@ -22,8 +22,10 @@ PASS = P * PACK
 HALF = 512
 QUADRANTS = 4
 LIST_COLS = S // 16
-STREAM_BUFS = 9
-WORK_BUFS = 31
+STREAM_BUFS = 10
+WORK_BUFS = 25
+QUARTER = 256
+SHIFT = 16
 
 
 def tile_list_advisor_disagreement_audit_kernel(
@@ -35,8 +37,8 @@ def tile_list_advisor_disagreement_audit_kernel(
         keep = ctx.enter_context(tc.tile_pool(name="keep", bufs=1))
         psum = ctx.enter_context(tc.psum_pool(name="psum", bufs=1))
 
-        def held(shape, dtype, name):
-            return keep.tile(shape, dtype, name=name, align_bytes=64)
+        def held(shape, dtype, name, tag=None):
+            return keep.tile(shape, dtype, name=name, tag=tag or name, align_bytes=64)
 
         def stream(shape, dtype, name):
             return keep.tile(shape, dtype, name=name, tag="stream", bufs=STREAM_BUFS, align_bytes=64)
@@ -44,115 +46,173 @@ def tile_list_advisor_disagreement_audit_kernel(
         def work(shape, dtype, name):
             return keep.tile(shape, dtype, name=name, tag="work", bufs=WORK_BUFS, align_bytes=64)
 
-        def half_cols(hf):
-            return slice(HALF * hf, HALF * (hf + 1))
-
-        def half_list(lst, hf):
-            return lst[:, LIST_COLS // 2 * hf : LIST_COLS // 2 * (hf + 1)]
+        def list_cols(lst, first, count):
+            return lst[:, first // 16 : (first + count) // 16]
 
         def group_rows(x, b):
             return x[PASS * b : PASS * (b + 1)].rearrange("(p t) c -> p t c", t=PACK)
 
         def quantise(woven, name):
-            codes = work([P, PASS], U32, name + "_codes")
+            words = woven.shape[1] // PACK
+            codes = work([P, words], U32, name + "_codes")
             if name == "wa1_0":
-                plane = lists.tile([P, PASS], U8, name=name + "_plane", tag="late_list", bufs=2, align_bytes=64)
+                plane = lists.tile([P, words], U8, name=name + "_plane", tag="late_list", bufs=2, align_bytes=64)
             else:
-                plane = held([P, PASS], U8, name + "_plane")
+                plane = held([P, words], U8, name + "_plane")
             nc.vector.quantize_mx(out=codes[:].bitcast(E4M3), scales=plane[:], in_=woven)
             return codes, plane
 
+        pages = {}
+
+        def clear_page(n, place):
+            pages[n] = place([P, T2], F32, "page%d" % n)
+            nc.vector.memset(pages[n][:], 0.0)
+
         tab_plane = held([P, T], U8, "tab_plane")
         tab = [stream([P, T], I32, "tab0")]
-        wb_plane = stream([P, 2, H], U8, "wb_plane")
-        tab.append(stream([P, T], I32, "tab1"))
-        v_words = [work([P, S], U32, "v_words0")]
-        v_planes = [work([P, S], U8, "v_plane0"), held([P, S], U8, "v_plane1")]
-        v_words.append(work([P, S], U32, "v_words1"))
-        pages = [held([P, T2], F32, "page%d" % n) for n in range(N // P)]
+        wb_plane = held([P, 2, H], U8, "wb_plane")
+        v_plane1 = held([P, S], U8, "v_plane1")
         nc.vector.memset(tab_plane[:].bitcast(I32), 0)
-        nc.vector.memset(pages[0][:], 0.0)
-        nc.vector.memset(v_planes[1][:].bitcast(I32), 0)
-        for page in pages[1:]:
-            nc.vector.memset(page[:], 0.0)
         nc.vector.memset(wb_plane[:].bitcast(I32), 0)
+        clear_page(0, stream)
+        nc.vector.memset(v_plane1[:].bitcast(I32), 0)
+        for n in range(1, N // P):
+            clear_page(n, held)
 
         idx = lists.tile([P, LIST_COLS], U16, name="idx")
         nc.sync.dma_start(idx[:], offs)
-        for q in (0, 2, 1, 3):
+        nc.sync.dma_start(out=tab[0][:], in_=tab_words[0].rearrange("p t i -> p (t i)").bitcast(I32))
+        for r in range(4):
             nc.sync.dma_start(
-                out=tab_plane[32 * q : 32 * q + 8, :].bitcast(I32), in_=tab_scales[:, 4 * q : 4 * q + 4, :].bitcast(I32)
+                out=tab_plane[r:P:SHIFT, :].bitcast(I32),
+                in_=tab_scales[:, r:16:4, :].rearrange("a q c -> q a c").bitcast(I32),
             )
-        for a in range(2):
-            nc.sync.dma_start(out=tab[a][:], in_=tab_words[a].rearrange("p t i -> p (t i)").bitcast(I32))
-        nc.vector.tensor_copy(v_planes[0][:], tab_plane[:].indirect(idx[:]))
-        live = 32 * (QUADRANTS - 1) + 4
-        nc.scalar.dma_start(out=v_planes[1][0:live, :].bitcast(I32), in_=v_planes[0][4 : live + 4, :].bitcast(I32))
         for q in (0, 2, 1, 3):
             nc.gpsimd.dma_start(
                 out=wb_plane[32 * q : 32 * q + 4, :, :].bitcast(I32),
                 in_=wb_scales[:, 4 * q : 4 * q + 4, :].rearrange("a r c -> r a c").bitcast(I32),
             )
-        for a in range(2):
+        v_words, v_planes = [], []
+
+        def pick_planes():
+            v_planes.extend([work([P, S], U8, "v_plane0"), v_plane1])
+            nc.vector.tensor_copy(v_planes[0][:], tab_plane[:].indirect(idx[:]))
+            for first in (0, P // 2):
+                nc.gpsimd.dma_start(
+                    out=v_planes[1][first : first + 36, :].bitcast(I32),
+                    in_=v_planes[0][first + SHIFT : first + SHIFT + 36, :].bitcast(I32),
+                )
+
+        def load_tab1():
+            tab.append(stream([P, T], I32, "tab1"))
+            nc.sync.dma_start(out=tab[1][:], in_=tab_words[1].rearrange("p t i -> p (t i)").bitcast(I32))
+
+        def pick_words(a):
+            v_words.append(work([P, S], U32, "v_words%d" % a))
             nc.vector.tensor_copy(v_words[a][:], tab[a][:].bitcast(U32).indirect(idx[:]))
 
-        rests = {}
-        s_rows, picked, slopes, wa_woven, wa_mx, wb_codes, signed_h = {}, {}, {}, {}, {}, {}, {}
-        wb_raw, w3_raw, w3_woven, w3_mx, h_woven, h_mx = {}, {}, {}, {}, {}, {}
+        s_rows, picked, partial, wa_woven, wa_mx, wb_codes, signed_h = {}, {}, {}, {}, {}, {}, {}
+        rests, slopes = {}, {}
+        wb_raw, w3_raw, w3_woven, w3_mx, h_woven, h_mx, banks, wb_planes = {}, {}, {}, {}, {}, {}, {}, {}
 
-        def load_s(b, t):
-            s_rows[b, t] = stream([P, T], F32, "s_rows%d_%d" % (b, t))
+        def load_s(b, t, tag=None):
+            name = "s_rows%d_%d" % (b, t)
+            s_rows[b, t] = held([P, T], F32, name, tag) if tag else stream([P, T], F32, name)
             nc.sync.dma_start(out=s_rows[b, t][:], in_=group_rows(sT, b)[:, t, :])
 
-        def pick(b, t, halves):
-            name = "%d_%d_%d" % (b, t, halves[0])
-            picked[b, t, halves] = work([P, HALF * len(halves)], F32, "picked" + name)
-            entries = idx[:] if len(halves) == 2 else half_list(idx, halves[0])
-            nc.vector.tensor_copy(picked[b, t, halves][:], s_rows[b, t][:].indirect(entries))
+        def pick(b, t, first, count):
+            tile = work([P, count], F32, "picked%d_%d_%d" % (b, t, first))
+            nc.vector.tensor_copy(tile[:], s_rows[b, t][:].indirect(list_cols(idx, first, count)))
+            for j in range(0, count, QUARTER):
+                picked[b, t, first + j] = (tile, j)
 
-        def rest(b, t, halves, over=None):
-            if over is None:
-                rests[b, t, halves] = work([P, HALF * len(halves)], F32, "rest%d_%d_%d" % (b, t, halves[0]))[:]
+        def multiply(b, t, hf):
+            bank = psum.tile([P, HALF], F32, name="d%d_%d_%d" % (b, hf, t), tag="bank%d_%d" % (hf, t))
+            banks[b, t, hf] = bank
+            cols = slice(P * t, P * (t + 1))
+            passes = [(wb_codes[b][:, a, cols], wb_planes[b][:, a, cols], a) for a in range(2)]
+            wa_passes = [(wa_mx[b, a][0][:, cols], wa_mx[b, a][1][:, cols], a) for a in range(2)]
+            if (b, t) == (0, 0):
+                passes = wa_passes[:1] + passes + wa_passes[1:]
+            elif b == 0:
+                passes = wa_passes[::-1] + passes
             else:
-                rests[b, t, halves] = over[:].rearrange("p c i -> p (c i)").bitcast(F32)
-            nc.scalar.activation(
-                out=rests[b, t, halves], in_=picked[b, t, halves][:], func=ACT.Copy, scale=-1.0, bias=1.0
+                passes = passes + wa_passes
+            entries = slice(HALF * hf, HALF * (hf + 1))
+            for number, (codes, plane, a) in enumerate(passes):
+                nc.tensor.matmul_mx(
+                    out=bank[:],
+                    lhsT=codes.bitcast(E4M3),
+                    lhsT_scale=plane,
+                    rhs=v_words[a][:, entries].bitcast(E5M2),
+                    rhs_scale=v_planes[a][:, entries],
+                    start=(number == 0),
+                    stop=(number == len(passes) - 1),
+                )
+
+        def weigh(b, t, first, count):
+            hf, within = divmod(first, HALF)
+            if (b, t, hf) not in banks:
+                multiply(b, t, hf)
+            tile, j = picked[b, t, first]
+            partial[b, t, first] = work([P, count], F32, "partial%d_%d_%d" % (b, t, first))
+            nc.vector.scalar_tensor_tensor(
+                out=partial[b, t, first][:],
+                in0=tile[:, j : j + count],
+                scalar=1.0,
+                in1=banks[b, t, hf][:, within : within + count],
+                op0=ALU.subtract,
+                op1=ALU.mult,
             )
 
-        def slope_half(b, t, hf, over=None):
-            if over is None:
-                made = work([P, HALF], F32, "slope%d_%d_%d" % (b, t, hf))[:]
-            else:
-                made = over[:].rearrange("p c i -> p (c i)").bitcast(F32)[:, 0:HALF]
+        def finish(b, t, first, count, engine):
+            hf, within = divmod(first, HALF)
+            if (b, hf) not in signed_h:
+                signed_h[b, hf] = held([P, PACK, HALF], BF16, "signed_h%d_%d" % (b, hf))
+            tile, j = picked[b, t, first]
+            engine.tensor_tensor(
+                out=signed_h[b, hf][:, t, within : within + count],
+                in0=partial[b, t, first][:],
+                in1=tile[:, j : j + count],
+                op=ALU.mult,
+            )
+
+        def rest(b, t, first, count):
+            tile, j = picked[b, t, first]
+            made = work([P, count], F32, "rest%d_%d_%d" % (b, t, first))
+            nc.scalar.activation(out=made[:], in_=tile[:, j : j + count], func=ACT.Copy, scale=-1.0, bias=1.0)
+            for k in range(0, count, QUARTER):
+                rests[b, t, first + k] = (made, k)
+
+        def slope(b, t, first, count):
+            tile, j = picked[b, t, first]
+            other, k = rests[b, t, first]
+            slopes[b, t, first] = work([P, count], F32, "slope%d_%d_%d" % (b, t, first))
             nc.gpsimd.tensor_tensor(
-                out=made, in0=rests[b, t, both][:, half_cols(hf)], in1=picked[b, t, both][:, half_cols(hf)], op=ALU.mult
-            )
-            slopes[b, t, hf] = made
-
-        def weave_h_part(b, hf, part):
-            if part == 0:
-                h_woven[b, hf] = work([P, HALF, PACK], BF16, "h_woven%d_%d" % (b, hf))
-            cols = slice(HALF // 2 * part, HALF // 2 * (part + 1))
-            nc.scalar.activation(
-                out=h_woven[b, hf][:, cols, :].rearrange("p (g e) t -> p g t e", e=4),
-                in_=signed_h[b, hf][:, :, cols].rearrange("p t (g e) -> p g t e", e=4),
-                func=ACT.Abs,
+                out=slopes[b, t, first][:], in0=other[:, k : k + count], in1=tile[:, j : j + count], op=ALU.mult
             )
 
-        def slope(b, t, halves, on_vector):
-            s = picked[b, t, halves][:]
-            made = work([P, HALF * len(halves)], F32, "slope%d_%d_%d" % (b, t, halves[0]))
-            if on_vector:
-                nc.vector.scalar_tensor_tensor(out=made[:], in0=s, scalar=1.0, in1=s, op0=ALU.subtract, op1=ALU.mult)
-            else:
-                nc.gpsimd.tensor_tensor(out=made[:], in0=rests[b, t, halves], in1=s, op=ALU.mult)
-            for place, hf in enumerate(halves):
-                slopes[b, t, hf] = made[:, half_cols(place)]
+        def product(b, t, first, count):
+            hf, within = divmod(first, HALF)
+            if (b, t, hf) not in banks:
+                multiply(b, t, hf)
+            if (b, hf) not in signed_h:
+                signed_h[b, hf] = held([P, PACK, HALF], BF16, "signed_h%d_%d" % (b, hf))
+            nc.vector.tensor_tensor(
+                out=signed_h[b, hf][:, t, within : within + count],
+                in0=banks[b, t, hf][:, within : within + count],
+                in1=slopes[b, t, first][:],
+                op=ALU.mult,
+            )
 
-        def weave_wa(b, a):
+        def load_wa(b, a):
             raw = stream([P, PACK, PASS], F32, "wa_raw%d_%d" % (b, a))
             nc.sync.dma_start(out=raw[:], in_=group_rows(wa[:, PASS * b : PASS * (b + 1)], a))
-            wa_woven[b, a] = work([P, PASS, PACK], BF16, "wa_woven%d_%d" % (b, a))
+            return raw
+
+        def weave_wa(b, a, raw, tag=None):
+            name = "wa_woven%d_%d" % (b, a)
+            wa_woven[b, a] = held([P, PASS, PACK], BF16, name, tag) if tag else work([P, PASS, PACK], BF16, name)
             nc.scalar.activation(
                 out=wa_woven[b, a][:].rearrange("p (t m) i -> p m i t", t=PACK),
                 in_=raw[:].rearrange("p i (m t) -> p m i t", t=PACK),
@@ -168,184 +228,177 @@ def tile_list_advisor_disagreement_audit_kernel(
             words = wb_words[:, :, PASS * b : PASS * (b + 1), :].rearrange("a p c i -> p a (c i)")
             nc.sync.dma_start(out=wb_raw[b][:], in_=words.bitcast(I32))
 
-        def order_wb(b):
+        def order_wb(b, engine):
             wb_codes[b] = work([P, 2, PASS], I32, "wb_codes%d" % b)
-            (nc.vector, nc.gpsimd)[b].tensor_copy(
+            engine.tensor_copy(
                 out=wb_codes[b][:].rearrange("p a (t g e) -> p a g t e", t=PACK, e=4),
                 in_=wb_raw[b][:].rearrange("p a (g e t) -> p a g t e", t=PACK, e=4),
             )
 
-        def order_wb_plane():
-            ordered = work([P, 2, H], U8, "wb_ordered_plane")
+        def order_wb_plane(b, tag=None):
+            name = "wb_ordered_plane%d" % b
+            wb_planes[b] = held([P, 2, PASS], U8, name, tag) if tag else work([P, 2, PASS], U8, name)
             nc.gpsimd.tensor_copy(
-                out=ordered[:].rearrange("p a (b t m) -> p (a b) t m", b=2, t=PACK),
-                in_=wb_plane[:].rearrange("p a (b m t) -> p (a b) t m", b=2, t=PACK),
+                out=wb_planes[b][:].rearrange("p a (t m) -> p a t m", t=PACK),
+                in_=wb_plane[:, :, PASS * b : PASS * (b + 1)].rearrange("p a (m t) -> p a t m", t=PACK),
             )
-            return ordered
 
         def load_w3(c):
             w3_raw[c] = stream([P, 2, PACK, N // 2], F32, "w3_raw%d" % c)
             for b in range(2):
                 nc.sync.dma_start(out=w3_raw[c][:, b], in_=group_rows(w3[:, N // 2 * c : N // 2 * (c + 1)], b))
 
-        def weave_w3(c):
-            w3_woven[c] = work([P, 2, N // 2, PACK], BF16, "w3_woven%d" % c)
+        def weave_w3(n):
+            w3_woven[n] = work([P, 2, P, PACK], BF16, "w3_woven%d" % n)
+            cols = slice(P * (n % 2), P * (n % 2 + 1))
             nc.scalar.copy(
-                out=w3_woven[c][:].rearrange("p b (g e) t -> p b g t e", e=4),
-                in_=w3_raw[c][:].rearrange("p b t (g e) -> p b g t e", e=4),
+                out=w3_woven[n][:].rearrange("p b (g e) t -> p b g t e", e=4),
+                in_=w3_raw[n // 2][:, :, :, cols].rearrange("p b t (g e) -> p b g t e", e=4),
             )
 
-        def quantise_w3(c):
-            w3_mx[c] = quantise(w3_woven[c][:].rearrange("p b n t -> p (b n t)"), "w3_%d" % c)
+        def quantise_w3(n):
+            codes, plane = quantise(w3_woven[n][:].rearrange("p b n t -> p (b n t)"), "w3_%d" % n)
+            for b in range(2):
+                w3_mx[n, b] = (codes[:, P * b : P * (b + 1)], plane[:, P * b : P * (b + 1)])
 
-        def weigh(b, hf, t):
-            if t == 0:
-                signed_h[b, hf] = work([P, PACK, HALF], BF16, "signed_h%d_%d" % (b, hf))
-            bank = psum.tile([P, HALF], F32, name="d%d_%d_%d" % (b, hf, t), tag="bank%d_%d" % (hf, t))
-            cols = slice(P * t, P * (t + 1))
-            cols_of_all = slice(PASS * b + P * t, PASS * b + P * (t + 1))
-            passes = [(wb_codes[b][:, a, cols], wb_ordered_plane[:, a, cols_of_all], a) for a in range(2)]
-            wa_passes = [(wa_mx[b, a][0][:, cols], wa_mx[b, a][1][:, cols], a) for a in range(2)]
-            if (b, t) == (0, 0):
-                passes = wa_passes[:1] + passes + wa_passes[1:]
-            elif b == 0:
-                passes = passes[::-1] + wa_passes[::-1]
-            elif t < PACK - 1:
-                passes = passes + wa_passes
-            else:
-                passes = wa_passes[::-1] + passes
-            for number, (codes, plane, a) in enumerate(passes):
-                nc.tensor.matmul_mx(
-                    out=bank[:],
-                    lhsT=codes.bitcast(E4M3),
-                    lhsT_scale=plane,
-                    rhs=v_words[a][:, half_cols(hf)].bitcast(E5M2),
-                    rhs_scale=v_planes[a][:, half_cols(hf)],
-                    start=(number == 0),
-                    stop=(number == len(passes) - 1),
-                )
-            nc.vector.tensor_tensor(out=signed_h[b, hf][:, t, :], in0=bank[:], in1=slopes[b, t, hf], op=ALU.mult)
-
-        def weave_h(b, hf):
-            h_woven[b, hf] = work([P, HALF, PACK], BF16, "h_woven%d_%d" % (b, hf))
+        def weave_h(b, first, count):
+            hf, within = divmod(first, HALF)
+            h_woven[b, first] = work([P, count, PACK], BF16, "h_woven%d_%d" % (b, first))
             nc.scalar.activation(
-                out=h_woven[b, hf][:].rearrange("p (g e) t -> p g t e", e=4),
-                in_=signed_h[b, hf][:].rearrange("p t (g e) -> p g t e", e=4),
+                out=h_woven[b, first][:].rearrange("p (g e) t -> p g t e", e=4),
+                in_=signed_h[b, hf][:, :, within : within + count].rearrange("p t (g e) -> p g t e", e=4),
                 func=ACT.Abs,
             )
 
-        def quantise_h(b, hf):
-            h_mx[b, hf] = quantise(h_woven[b, hf][:].rearrange("p j t -> p (j t)"), "h%d_%d" % (b, hf))
+        def quantise_h(b, first, count):
+            codes, plane = quantise(h_woven[b, first][:].rearrange("p j t -> p (j t)"), "h%d_%d" % (b, first))
+            for j in range(0, count, QUARTER):
+                h_mx[b, first + j] = (codes, plane, j, count - j)
 
-        def audit(hf, n):
-            bank = psum.tile([P, HALF], F32, name="y%d_%d" % (hf, n), tag="bank%d_%d" % (hf, n))
+        def audit(n, first, count):
+            hf = first // HALF
+            bank = psum.tile([P, count], F32, name="y%d_%d" % (n, first), tag="bank%d_%d" % (hf, n))
+            passes = []
             for b in range(2):
-                cols = slice(N // 2 * b + P * (n % 2), N // 2 * b + P * (n % 2 + 1))
+                done = 0
+                while done < count:
+                    codes, plane, j, left = h_mx[b, first + done]
+                    width = min(left, count - done)
+                    passes.append((b, done, width, codes[:, j : j + width], plane[:, j : j + width]))
+                    done = done + width
+            for number, (b, start, width, codes, plane) in enumerate(passes):
                 nc.tensor.matmul_mx(
-                    out=bank[:],
-                    lhsT=w3_mx[n // 2][0][:, cols].bitcast(E4M3),
-                    lhsT_scale=w3_mx[n // 2][1][:, cols],
-                    rhs=h_mx[b, hf][0][:].bitcast(E4M3),
-                    rhs_scale=h_mx[b, hf][1][:],
-                    start=(b == 0),
-                    stop=(b == 1),
+                    out=bank[:, start : start + width],
+                    lhsT=w3_mx[n, b][0].bitcast(E4M3),
+                    lhsT_scale=w3_mx[n, b][1],
+                    rhs=codes.bitcast(E4M3),
+                    rhs_scale=plane,
+                    start=(number == 0),
+                    stop=(number == len(passes) - 1),
                 )
-            y = work([P, HALF], F32, "y_sb%d_%d" % (hf, n))
+            y = work([P, count], F32, "y_sb%d_%d" % (n, first))
             nc.scalar.copy(out=y[:], in_=bank[:])
-            nc.vector.tensor_tensor(pages[n][:].indirect(half_list(idx2, hf)), y[:], gains[:, half_cols(hf)], ALU.mult)
-            if hf == 1:
+            nc.vector.tensor_tensor(
+                pages[n][:].indirect(list_cols(idx2, first, count)), y[:], gains[:, first : first + count], ALU.mult
+            )
+            if first + count == S:
                 nc.sync.dma_start(out=out[P * n : P * (n + 1), :], in_=pages[n][:])
 
-        both = (0, 1)
-        load_s(0, 0)
-        pick(0, 0, both)
-        weave_wa(0, 0)
-        load_s(0, 1)
-        pick(0, 1, both)
+        V, G = nc.vector, nc.gpsimd
+        both = (0, HALF)
+
+        def weigh_both(b, t):
+            for first in both:
+                weigh(b, t, first, HALF)
+                finish(b, t, first, HALF, G)
+
+        def weigh_half(b, t, first):
+            weigh(b, t, first, HALF)
+            finish(b, t, first, HALF, G)
+
+        pick_words(0)
+        pick_planes()
+        weave_wa(0, 0, load_wa(0, 0))
+        load_tab1()
+        pick_words(1)
+        order_wb_plane(0)
         quantise_wa(0, 0)
-        slope(0, 0, both, True)
-        weave_wa(0, 1)
-        wb_ordered_plane = order_wb_plane()
+        weave_wa(0, 1, load_wa(0, 1), "after_wa01")
         load_wb(0)
-        order_wb(0)
+        order_wb(0, V)
         quantise_wa(0, 1)
-        rest(0, 1, both, wa_woven[0, 1])
-        load_s(0, 2)
-        pick(0, 2, both)
+        load_s(0, 0)
+        pick(0, 0, 0, S)
+        order_wb_plane(1, "after_wa01")
         load_wb(1)
-        order_wb(1)
-        rest(0, 2, both)
-        for hf in range(2):
-            weigh(0, hf, 0)
+        order_wb(1, G)
+        weigh_both(0, 0)
+        load_s(0, 1)
+        pick(0, 1, 0, S)
+        weigh_both(0, 1)
+        load_s(0, 2)
+        pick(0, 2, 0, S)
+        raw = load_wa(1, 0)
+        weigh_both(0, 2)
+        weave_wa(1, 0, raw)
         load_s(0, 3)
-        pick(0, 3, both)
-        slope(0, 1, both, False)
-        rest(0, 3, both)
-        for hf in range(2):
-            weigh(0, hf, 1)
-        load_s(1, 0)
-        pick(1, 0, both)
-        slope(0, 2, both, False)
-        weave_wa(1, 0)
-        for hf in range(2):
-            weigh(0, hf, 2)
+        pick(0, 3, 0, S)
         quantise_wa(1, 0)
-        rest(1, 0, both, wa_woven[1, 0])
-        load_s(1, 1)
-        pick(1, 1, both)
-        slope(0, 3, both, False)
-        slope_half(1, 0, 0)
-        for hf in range(2):
-            weigh(0, hf, 3)
-        weave_wa(1, 1)
+        weave_wa(1, 1, load_wa(1, 1))
+        weigh_both(0, 3)
+        load_s(1, 0)
+        pick(1, 0, 0, S)
         quantise_wa(1, 1)
-        weave_h_part(0, 0, 0)
-        rest(1, 1, both)
+        weave_h(0, 0, HALF)
+        load_s(1, 1)
+        pick(1, 1, 0, HALF)
+        weigh(1, 0, 0, HALF)
+        quantise_h(0, 0, HALF)
+        finish(1, 0, 0, HALF, G)
+        weigh_half(1, 0, HALF)
+        weave_h(0, HALF, HALF)
         load_s(1, 2)
-        pick(1, 2, (0,))
-        slope_half(1, 0, 1, wa_woven[1, 1])
-        rest(1, 2, (0,))
-        weigh(1, 0, 0)
+        pick(1, 2, 0, HALF)
+        weigh_half(1, 1, 0)
         load_s(1, 3)
-        pick(1, 3, (0,))
-        weave_h_part(0, 0, 1)
-        rest(1, 3, (0,))
-        pick(1, 2, (1,))
-        slope_half(1, 1, 0)
-        weigh(1, 0, 1)
-        slope(1, 2, (0,), False)
-        slope(1, 3, (0,), False)
-        pick(1, 3, (1,))
-        slope_half(1, 1, 1)
-        load_w3(0)
-        weave_w3(0)
-        rest(1, 2, (1,))
-        slope(1, 2, (1,), False)
-        idx2 = lists.tile([P, LIST_COLS], U16, name="idx2", tag="late_list", bufs=2, align_bytes=64)
-        nc.sync.dma_start(idx2[:], offs2)
         gains = stream([P, S], F32, "gains")
         nc.sync.dma_start(out=gains[:], in_=wgo)
+        load_w3(0)
         load_w3(1)
-        for t in range(2, PACK):
-            weigh(1, 0, t)
-        weave_h(1, 0)
-        weigh(1, 1, 0)
-        weigh(1, 1, 1)
-        quantise_h(0, 0)
+        idx2 = lists.tile([P, LIST_COLS], U16, name="idx2", tag="late_list", bufs=2, align_bytes=64)
+        nc.sync.dma_start(idx2[:], offs2)
+        pick(1, 3, 0, HALF)
+        weigh_half(1, 2, 0)
+        pick(1, 1, HALF, HALF)
+        weigh_half(1, 3, 0)
+        weigh_half(1, 1, HALF)
+        weave_w3(0)
+        pick(1, 2, HALF, HALF)
+        pick(1, 3, HALF, QUARTER)
+        weave_h(1, 0, QUARTER)
+        weigh_half(1, 2, HALF)
+        pick(1, 3, HALF + QUARTER, QUARTER)
+        weave_h(1, QUARTER, QUARTER)
+        weigh(1, 3, HALF, QUARTER)
+        weigh(1, 3, HALF + QUARTER, QUARTER)
         quantise_w3(0)
-        quantise_h(1, 0)
-        slope(1, 3, (1,), True)
-        weigh(1, 1, 2)
-        weigh(1, 1, 3)
-        audit(0, 0)
+        quantise_h(1, 0, QUARTER)
         weave_w3(1)
+        quantise_h(1, QUARTER, QUARTER)
+        quantise_h(0, HALF, HALF)
+        finish(1, 3, HALF, QUARTER, V)
+        finish(1, 3, HALF + QUARTER, QUARTER, V)
+        audit(0, 0, QUARTER)
+        audit(0, QUARTER, QUARTER)
         quantise_w3(1)
-        audit(0, 1)
-        weave_h(0, 1)
-        quantise_h(0, 1)
-        audit(0, 2)
-        weave_h(1, 1)
-        quantise_h(1, 1)
-        audit(0, 3)
+        weave_w3(2)
+        audit(1, 0, HALF)
+        quantise_w3(2)
+        weave_w3(3)
+        weave_h(1, HALF, HALF)
+        audit(2, 0, HALF)
+        quantise_w3(3)
+        quantise_h(1, HALF, HALF)
+        audit(3, 0, HALF)
         for n in range(N // P):
-            audit(1, n)
+            audit(n, HALF, HALF)

@@ -22,8 +22,9 @@ PASS = P * PACK
 HALF = 512
 QUADRANTS = 4
 LIST_COLS = S // 16
+FUSED = ((0, 2, 0), (0, 2, 1), (0, 3, 0), (0, 3, 1), (1, 3, 1))
 STREAM_BUFS = 10
-WORK_BUFS = 25
+WORK_BUFS = 26
 QUARTER = 256
 SHIFT = 16
 
@@ -156,6 +157,14 @@ def tile_list_advisor_disagreement_audit_kernel(
                 multiply(b, t, hf)
             tile, j = picked[b, t, first]
             partial[b, t, first] = work([P, count], F32, "partial%d_%d_%d" % (b, t, first))
+            if (b, t, first // HALF) not in FUSED:
+                nc.vector.tensor_tensor(
+                    out=partial[b, t, first][:],
+                    in0=banks[b, t, hf][:, within : within + count],
+                    in1=tile[:, j : j + count],
+                    op=ALU.mult,
+                )
+                return
             nc.vector.scalar_tensor_tensor(
                 out=partial[b, t, first][:],
                 in0=tile[:, j : j + count],
@@ -169,7 +178,7 @@ def tile_list_advisor_disagreement_audit_kernel(
             hf, within = divmod(first, HALF)
             if (b, hf) not in signed_h:
                 signed_h[b, hf] = held([P, PACK, HALF], BF16, "signed_h%d_%d" % (b, hf))
-            tile, j = picked[b, t, first]
+            tile, j = rests.get((b, t, first), picked[b, t, first])
             engine.tensor_tensor(
                 out=signed_h[b, hf][:, t, within : within + count],
                 in0=partial[b, t, first][:],
@@ -277,7 +286,7 @@ def tile_list_advisor_disagreement_audit_kernel(
 
         def audit(n, first, count):
             hf = first // HALF
-            bank = psum.tile([P, count], F32, name="y%d_%d" % (n, first), tag="bank%d_%d" % (hf, n))
+            bank = psum.tile([P, count], F32, name="y%d_%d" % (n, first), tag="bank%d_%d" % (hf, n if first % HALF == 0 else PACK - 1))
             passes = []
             for b in range(2):
                 done = 0
@@ -329,12 +338,14 @@ def tile_list_advisor_disagreement_audit_kernel(
         quantise_wa(0, 1)
         load_s(0, 0)
         pick(0, 0, 0, S)
+        rest(0, 0, 0, S)
         order_wb_plane(1, "after_wa01")
+        load_s(0, 1)
+        pick(0, 1, 0, S)
+        rest(0, 1, 0, S)
         load_wb(1)
         order_wb(1, G)
         weigh_both(0, 0)
-        load_s(0, 1)
-        pick(0, 1, 0, S)
         weigh_both(0, 1)
         load_s(0, 2)
         pick(0, 2, 0, S)
@@ -350,6 +361,7 @@ def tile_list_advisor_disagreement_audit_kernel(
         pick(1, 0, 0, S)
         quantise_wa(1, 1)
         weave_h(0, 0, HALF)
+        rest(1, 0, 0, S)
         load_s(1, 1)
         pick(1, 1, 0, HALF)
         weigh(1, 0, 0, HALF)
@@ -358,7 +370,9 @@ def tile_list_advisor_disagreement_audit_kernel(
         weigh_half(1, 0, HALF)
         weave_h(0, HALF, HALF)
         load_s(1, 2)
+        rest(1, 1, 0, HALF)
         pick(1, 2, 0, HALF)
+        rest(1, 2, 0, HALF)
         weigh_half(1, 1, 0)
         load_s(1, 3)
         gains = stream([P, S], F32, "gains")
@@ -368,32 +382,32 @@ def tile_list_advisor_disagreement_audit_kernel(
         idx2 = lists.tile([P, LIST_COLS], U16, name="idx2", tag="late_list", bufs=2, align_bytes=64)
         nc.sync.dma_start(idx2[:], offs2)
         pick(1, 3, 0, HALF)
+        rest(1, 3, 0, HALF)
         weigh_half(1, 2, 0)
         pick(1, 1, HALF, HALF)
         weigh_half(1, 3, 0)
-        weigh_half(1, 1, HALF)
+        rest(1, 1, HALF, HALF)
         weave_w3(0)
         pick(1, 2, HALF, HALF)
-        pick(1, 3, HALF, QUARTER)
+        rest(1, 2, HALF, HALF)
         weave_h(1, 0, QUARTER)
+        weigh_half(1, 1, HALF)
         weigh_half(1, 2, HALF)
-        pick(1, 3, HALF + QUARTER, QUARTER)
         weave_h(1, QUARTER, QUARTER)
-        weigh(1, 3, HALF, QUARTER)
-        weigh(1, 3, HALF + QUARTER, QUARTER)
+        pick(1, 3, HALF, HALF)
+        weigh(1, 3, HALF, HALF)
         quantise_w3(0)
         quantise_h(1, 0, QUARTER)
         weave_w3(1)
         quantise_h(1, QUARTER, QUARTER)
+        finish(1, 3, HALF, HALF, V)
         quantise_h(0, HALF, HALF)
-        finish(1, 3, HALF, QUARTER, V)
-        finish(1, 3, HALF + QUARTER, QUARTER, V)
-        audit(0, 0, QUARTER)
-        audit(0, QUARTER, QUARTER)
         quantise_w3(1)
+        audit(0, 0, QUARTER)
         weave_w3(2)
-        audit(1, 0, HALF)
+        audit(0, QUARTER, QUARTER)
         quantise_w3(2)
+        audit(1, 0, HALF)
         weave_w3(3)
         weave_h(1, HALF, HALF)
         audit(2, 0, HALF)

@@ -74,11 +74,12 @@ def tile_list_advisor_disagreement_audit_kernel(
         wb_plane = held([P, 2, H], U8, "wb_plane")
         v_plane1 = held([P, S], U8, "v_plane1")
         nc.vector.memset(tab_plane[:].bitcast(I32), 0)
-        nc.vector.memset(wb_plane[:].bitcast(I32), 0)
-        clear_page(0, stream)
+        clear_page(0, held)
         nc.vector.memset(v_plane1[:].bitcast(I32), 0)
-        for n in range(1, N // P):
-            clear_page(n, held)
+        clear_page(1, stream)
+        clear_page(2, held)
+        clear_page(3, held)
+        nc.vector.memset(wb_plane[:].bitcast(I32), 0)
 
         idx = lists.tile([P, LIST_COLS], U16, name="idx")
         nc.sync.dma_start(idx[:], offs)
@@ -244,12 +245,12 @@ def tile_list_advisor_disagreement_audit_kernel(
                 in_=wb_raw[b][:].rearrange("p a (g e t) -> p a g t e", t=PACK, e=4),
             )
 
-        def order_wb_plane(b, tag=None):
+        def order_wb_plane(b, engine, tag=None):
             name = "wb_ordered_plane%d" % b
             wb_planes[b] = held([P, 2, PASS], U8, name, tag) if tag else work([P, 2, PASS], U8, name)
-            nc.gpsimd.tensor_copy(
-                out=wb_planes[b][:].rearrange("p a (t m) -> p a t m", t=PACK),
-                in_=wb_plane[:, :, PASS * b : PASS * (b + 1)].rearrange("p a (m t) -> p a t m", t=PACK),
+            engine.tensor_copy(
+                out=wb_planes[b][:].rearrange("p a (t g e) -> p a g t e", t=PACK, e=16),
+                in_=wb_plane[:, :, PASS * b : PASS * (b + 1)].rearrange("p a (g e t) -> p a g t e", t=PACK, e=16),
             )
 
         def load_w3(c):
@@ -330,8 +331,8 @@ def tile_list_advisor_disagreement_audit_kernel(
         weave_wa(0, 0, load_wa(0, 0))
         load_tab1()
         pick_words(1)
-        order_wb_plane(0)
         quantise_wa(0, 0)
+        order_wb_plane(0, V)
         weave_wa(0, 1, load_wa(0, 1), "after_wa01")
         load_wb(0)
         order_wb(0, V)
@@ -339,7 +340,7 @@ def tile_list_advisor_disagreement_audit_kernel(
         load_s(0, 0)
         pick(0, 0, 0, S)
         rest(0, 0, 0, S)
-        order_wb_plane(1, "after_wa01")
+        order_wb_plane(1, G, "after_wa01")
         load_s(0, 1)
         pick(0, 1, 0, S)
         rest(0, 1, 0, S)

@@ -89,10 +89,10 @@ def tile_list_advisor_disagreement_audit_kernel(
                 out=tab_plane[r:P:SHIFT, :].bitcast(I32),
                 in_=tab_scales[:, r:16:4, :].rearrange("a q c -> q a c").bitcast(I32),
             )
-        for q in (0, 2, 1, 3):
+        for r in range(4):
             nc.gpsimd.dma_start(
-                out=wb_plane[32 * q : 32 * q + 4, :, :].bitcast(I32),
-                in_=wb_scales[:, 4 * q : 4 * q + 4, :].rearrange("a r c -> r a c").bitcast(I32),
+                out=wb_plane[r:P:32, :, :].bitcast(I32),
+                in_=wb_scales[:, r:16:4, :].rearrange("a q c -> q a c").bitcast(I32),
             )
         v_words, v_planes = [], []
 

@@ -230,6 +230,16 @@ def tile_list_advisor_disagreement_audit_kernel(
                 scale=-1.0,
             )
 
+        def weave_wa_shared(b, a, raw, tag):
+            woven = held([P, PASS, PACK], BF16, "wa_woven%d_%d" % (b, a), tag)
+            wa_woven[b, a] = woven
+            columns = woven[:].rearrange("p (t m) i -> p m i t", t=PACK)
+            rows = raw[:].rearrange("p i (m t) -> p m i t", t=PACK)
+            nc.scalar.activation(out=columns[:, P // 2 :], in_=rows[:, P // 2 :], func=ACT.Copy, scale=-1.0)
+            nc.vector.tensor_scalar(
+                out=columns[:, : P // 2], in0=rows[:, : P // 2], scalar1=-1.0, scalar2=None, op0=ALU.mult
+            )
+
         def quantise_wa(b, a):
             wa_mx[b, a] = quantise(wa_woven[b, a][:].rearrange("p c i -> p (c i)"), "wa%d_%d" % (b, a))
 
@@ -332,9 +342,9 @@ def tile_list_advisor_disagreement_audit_kernel(
         load_tab1()
         pick_words(1)
         quantise_wa(0, 0)
-        order_wb_plane(0, V)
-        weave_wa(0, 1, load_wa(0, 1), "after_wa01")
+        weave_wa_shared(0, 1, load_wa(0, 1), "after_wa01")
         load_wb(0)
+        order_wb_plane(0, V)
         order_wb(0, V)
         quantise_wa(0, 1)
         load_s(0, 0)

from contextlib import ExitStack

import concourse.mybir as mybir

K, T, S, H, N, T2 = 1024, 2048, 1024, 1024, 512, 2048
FLOPS = 2 * (2 * K * H * S + H * N * S)

F32 = mybir.dt.float32
BF16 = mybir.dt.bfloat16
I32 = mybir.dt.int32
U32 = mybir.dt.uint32
U16 = mybir.dt.uint16
U8 = mybir.dt.uint8
E4M3 = mybir.dt.float8_e4m3fn_x4
E5M2 = mybir.dt.float8_e5m2_x4
ALU = mybir.AluOpType
ACT = mybir.ActivationFunctionType

P = 128
PACK = 4
PASS = P * PACK
HALF = 512
QUADRANTS = 4
LIST_COLS = S // 16
FUSED = ((0, 2, 0), (0, 2, 1), (0, 3, 0), (0, 3, 1), (1, 3, 1))
STREAM_BUFS = 10
WORK_BUFS = 26
QUARTER = 256
SHIFT = 16


def tile_list_advisor_disagreement_audit_kernel(
    tc, tab_words, tab_scales, offs, wa, wb_words, wb_scales, sT, w3, wgo, offs2, out
):
    nc = tc.nc
    with ExitStack() as ctx:
        lists = ctx.enter_context(tc.tile_pool(name="lists", bufs=1))
        keep = ctx.enter_context(tc.tile_pool(name="keep", bufs=1))
        psum = ctx.enter_context(tc.psum_pool(name="psum", bufs=1))

        def held(shape, dtype, name, tag=None):
            return keep.tile(shape, dtype, name=name, tag=tag or name, align_bytes=64)

        def stream(shape, dtype, name):
            return keep.tile(shape, dtype, name=name, tag="stream", bufs=STREAM_BUFS, align_bytes=64)

        def work(shape, dtype, name):
            return keep.tile(shape, dtype, name=name, tag="work", bufs=WORK_BUFS, align_bytes=64)

        def list_cols(lst, first, count):
            return lst[:, first // 16 : (first + count) // 16]

        def group_rows(x, b):
            return x[PASS * b : PASS * (b + 1)].rearrange("(p t) c -> p t c", t=PACK)

        def quantise(woven, name):
            words = woven.shape[1] // PACK
            codes = work([P, words], U32, name + "_codes")
            if name == "wa1_0":
                plane = lists.tile([P, words], U8, name=name + "_plane", tag="late_list", bufs=2, align_bytes=64)
            else:
                plane = held([P, words], U8, name + "_plane")
            nc.vector.quantize_mx(out=codes[:].bitcast(E4M3), scales=plane[:], in_=woven)
            return codes, plane

        pages = {}

        def clear_page(n, place):
            pages[n] = place([P, T2], F32, "page%d" % n)
            nc.vector.memset(pages[n][:], 0.0)

        tab_plane = held([P, T], U8, "tab_plane")
        tab = [stream([P, T], I32, "tab0")]
        wb_plane = held([P, 2, H], U8, "wb_plane")
        v_plane1 = held([P, S], U8, "v_plane1")
        nc.vector.memset(tab_plane[:].bitcast(I32), 0)
        clear_page(0, held)
        nc.vector.memset(v_plane1[:].bitcast(I32), 0)
        clear_page(1, stream)
        clear_page(2, held)
        clear_page(3, held)
        nc.vector.memset(wb_plane[:].bitcast(I32), 0)

        idx = lists.tile([P, LIST_COLS], U16, name="idx")
        nc.sync.dma_start(idx[:], offs)
        nc.sync.dma_start(out=tab[0][:], in_=tab_words[0].rearrange("p t i -> p (t i)").bitcast(I32))
        for r in range(4):
            nc.sync.dma_start(
                out=tab_plane[r:P:SHIFT, :].bitcast(I32),
                in_=tab_scales[:, r:16:4, :].rearrange("a q c -> q a c").bitcast(I32),
            )
        for r in range(4):
            nc.gpsimd.dma_start(
                out=wb_plane[r:P:32, :, :].bitcast(I32),
                in_=wb_scales[:, r:16:4, :].rearrange("a q c -> q a c").bitcast(I32),
            )
        v_words, v_planes = [], []

        def pick_planes():
            v_planes.extend([work([P, S], U8, "v_plane0"), v_plane1])
            nc.vector.tensor_copy(v_planes[0][:], tab_plane[:].indirect(idx[:]))
            for first in (0, P // 2):
                nc.gpsimd.dma_start(
                    out=v_planes[1][first : first + 36, :].bitcast(I32),
                    in_=v_planes[0][first + SHIFT : first + SHIFT + 36, :].bitcast(I32),
                )

        def load_tab1():
            tab.append(stream([P, T], I32, "tab1"))
            nc.sync.dma_start(out=tab[1][:], in_=tab_words[1].rearrange("p t i -> p (t i)").bitcast(I32))

        def pick_words(a):
            v_words.append(work([P, S], U32, "v_words%d" % a))
            nc.vector.tensor_copy(v_words[a][:], tab[a][:].bitcast(U32).indirect(idx[:]))

        s_rows, picked, partial, wa_woven, wa_mx, wb_codes, signed_h = {}, {}, {}, {}, {}, {}, {}
        rests, slopes = {}, {}
        wb_raw, w3_raw, w3_woven, w3_mx, h_woven, h_mx, banks, wb_planes = {}, {}, {}, {}, {}, {}, {}, {}

        def load_s(b, t, tag=None):
            name = "s_rows%d_%d" % (b, t)
            s_rows[b, t] = held([P, T], F32, name, tag) if tag else stream([P, T], F32, name)
            nc.sync.dma_start(out=s_rows[b, t][:], in_=group_rows(sT, b)[:, t, :])

        def pick(b, t, first, count):
            tile = work([P, count], F32, "picked%d_%d_%d" % (b, t, first))
            nc.vector.tensor_copy(tile[:], s_rows[b, t][:].indirect(list_cols(idx, first, count)))
            for j in range(0, count, QUARTER):
                picked[b, t, first + j] = (tile, j)

        def multiply(b, t, hf):
            bank = psum.tile([P, HALF], F32, name="d%d_%d_%d" % (b, hf, t), tag="bank%d_%d" % (hf, t))
            banks[b, t, hf] = bank
            cols = slice(P * t, P * (t + 1))
            passes = [(wb_codes[b][:, a, cols], wb_planes[b][:, a, cols], a) for a in range(2)]
            wa_passes = [(wa_mx[b, a][0][:, cols], wa_mx[b, a][1][:, cols], a) for a in range(2)]
            if (b, t) == (0, 0):
                passes = wa_passes[:1] + passes + wa_passes[1:]
            elif b == 0:
                passes = wa_passes[::-1] + passes
            else:
                passes = passes + wa_passes
            entries = slice(HALF * hf, HALF * (hf + 1))
            for number, (codes, plane, a) in enumerate(passes):
                nc.tensor.matmul_mx(
                    out=bank[:],
                    lhsT=codes.bitcast(E4M3),
                    lhsT_scale=plane,
                    rhs=v_words[a][:, entries].bitcast(E5M2),
                    rhs_scale=v_planes[a][:, entries],
                    start=(number == 0),
                    stop=(number == len(passes) - 1),
                )

        def weigh(b, t, first, count):
            hf, within = divmod(first, HALF)
            if (b, t, hf) not in banks:
                multiply(b, t, hf)
            tile, j = picked[b, t, first]
            partial[b, t, first] = work([P, count], F32, "partial%d_%d_%d" % (b, t, first))
            if (b, t, first // HALF) not in FUSED:
                nc.vector.tensor_tensor(
                    out=partial[b, t, first][:],
                    in0=banks[b, t, hf][:, within : within + count],
                    in1=tile[:, j : j + count],
                    op=ALU.mult,
                )
                return
            nc.vector.scalar_tensor_tensor(
                out=partial[b, t, first][:],
                in0=tile[:, j : j + count],
                scalar=1.0,
                in1=banks[b, t, hf][:, within : within + count],
                op0=ALU.subtract,
                op1=ALU.mult,
            )

        def finish(b, t, first, count, engine):
            hf, within = divmod(first, HALF)
            if (b, hf) not in signed_h:
                signed_h[b, hf] = held([P, PACK, HALF], BF16, "signed_h%d_%d" % (b, hf))
            tile, j = rests.get((b, t, first), picked[b, t, first])
            engine.tensor_tensor(
                out=signed_h[b, hf][:, t, within : within + count],
                in0=partial[b, t, first][:],
                in1=tile[:, j : j + count],
                op=ALU.mult,
            )

        def rest(b, t, first, count):
            tile, j = picked[b, t, first]
            made = work([P, count], F32, "rest%d_%d_%d" % (b, t, first))
            nc.scalar.activation(out=made[:], in_=tile[:, j : j + count], func=ACT.Copy, scale=-1.0, bias=1.0)
            for k in range(0, count, QUARTER):
                rests[b, t, first + k] = (made, k)

        def slope(b, t, first, count):
            tile, j = picked[b, t, first]
            other, k = rests[b, t, first]
            slopes[b, t, first] = work([P, count], F32, "slope%d_%d_%d" % (b, t, first))
            nc.gpsimd.tensor_tensor(
                out=slopes[b, t, first][:], in0=other[:, k : k + count], in1=tile[:, j : j + count], op=ALU.mult
            )

        def product(b, t, first, count):
            hf, within = divmod(first, HALF)
            if (b, t, hf) not in banks:
                multiply(b, t, hf)
            if (b, hf) not in signed_h:
                signed_h[b, hf] = held([P, PACK, HALF], BF16, "signed_h%d_%d" % (b, hf))
            nc.vector.tensor_tensor(
                out=signed_h[b, hf][:, t, within : within + count],
                in0=banks[b, t, hf][:, within : within + count],
                in1=slopes[b, t, first][:],
                op=ALU.mult,
            )

        def load_wa(b, a):
            raw = stream([P, PACK, PASS], F32, "wa_raw%d_%d" % (b, a))
            nc.sync.dma_start(out=raw[:], in_=group_rows(wa[:, PASS * b : PASS * (b + 1)], a))
            return raw

        def weave_wa(b, a, raw, tag=None):
            name = "wa_woven%d_%d" % (b, a)
            wa_woven[b, a] = held([P, PASS, PACK], BF16, name, tag) if tag else work([P, PASS, PACK], BF16, name)
            nc.scalar.activation(
                out=wa_woven[b, a][:].rearrange("p (t m) i -> p m i t", t=PACK),
                in_=raw[:].rearrange("p i (m t) -> p m i t", t=PACK),
                func=ACT.Copy,
                scale=-1.0,
            )

        def weave_wa_shared(b, a, raw, tag):
            woven = held([P, PASS, PACK], BF16, "wa_woven%d_%d" % (b, a), tag)
            wa_woven[b, a] = woven
            columns = woven[:].rearrange("p (t m) i -> p m i t", t=PACK)
            rows = raw[:].rearrange("p i (m t) -> p m i t", t=PACK)
            nc.scalar.activation(out=columns[:, P // 2 :], in_=rows[:, P // 2 :], func=ACT.Copy, scale=-1.0)
            nc.vector.tensor_scalar(
                out=columns[:, : P // 2], in0=rows[:, : P // 2], scalar1=-1.0, scalar2=None, op0=ALU.mult
            )

        def quantise_wa(b, a):
            wa_mx[b, a] = quantise(wa_woven[b, a][:].rearrange("p c i -> p (c i)"), "wa%d_%d" % (b, a))

        def load_wb(b):
            wb_raw[b] = stream([P, 2, PASS], I32, "wb_raw%d" % b)
            words = wb_words[:, :, PASS * b : PASS * (b + 1), :].rearrange("a p c i -> p a (c i)")
            nc.sync.dma_start(out=wb_raw[b][:], in_=words.bitcast(I32))

        def order_wb(b, engine):
            wb_codes[b] = work([P, 2, PASS], I32, "wb_codes%d" % b)
            engine.tensor_copy(
                out=wb_codes[b][:].rearrange("p a (t g e) -> p a g t e", t=PACK, e=4),
                in_=wb_raw[b][:].rearrange("p a (g e t) -> p a g t e", t=PACK, e=4),
            )

        def order_wb_plane(b, engine, tag=None):
            name = "wb_ordered_plane%d" % b
            wb_planes[b] = held([P, 2, PASS], U8, name, tag) if tag else work([P, 2, PASS], U8, name)
            engine.tensor_copy(
                out=wb_planes[b][:].rearrange("p a (t g e) -> p a g t e", t=PACK, e=16),
                in_=wb_plane[:, :, PASS * b : PASS * (b + 1)].rearrange("p a (g e t) -> p a g t e", t=PACK, e=16),
            )

        def load_w3(c):
            w3_raw[c] = stream([P, 2, PACK, N // 2], F32, "w3_raw%d" % c)
            for b in range(2):
                nc.sync.dma_start(out=w3_raw[c][:, b], in_=group_rows(w3[:, N // 2 * c : N // 2 * (c + 1)], b))

        def weave_w3(n):
            w3_woven[n] = work([P, 2, P, PACK], BF16, "w3_woven%d" % n)
            cols = slice(P * (n % 2), P * (n % 2 + 1))
            nc.scalar.copy(
                out=w3_woven[n][:].rearrange("p b (g e) t -> p b g t e", e=4),
                in_=w3_raw[n // 2][:, :, :, cols].rearrange("p b t (g e) -> p b g t e", e=4),
            )

        def quantise_w3(n):
            codes, plane = quantise(w3_woven[n][:].rearrange("p b n t -> p (b n t)"), "w3_%d" % n)
            for b in range(2):
                w3_mx[n, b] = (codes[:, P * b : P * (b + 1)], plane[:, P * b : P * (b + 1)])

        def weave_h(b, first, count):
            hf, within = divmod(first, HALF)
            h_woven[b, first] = work([P, count, PACK], BF16, "h_woven%d_%d" % (b, first))
            nc.scalar.activation(
                out=h_woven[b, first][:].rearrange("p (g e) t -> p g t e", e=4),
                in_=signed_h[b, hf][:, :, within : within + count].rearrange("p t (g e) -> p g t e", e=4),
                func=ACT.Abs,
            )

        def quantise_h(b, first, count):
            codes, plane = quantise(h_woven[b, first][:].rearrange("p j t -> p (j t)"), "h%d_%d" % (b, first))
            for j in range(0, count, QUARTER):
                h_mx[b, first + j] = (codes, plane, j, count - j)

        def audit(n, first, count):
            hf = first // HALF
            bank = psum.tile([P, count], F32, name="y%d_%d" % (n, first), tag="bank%d_%d" % (hf, n if first % HALF == 0 else PACK - 1))
            passes = []
            for b in range(2):
                done = 0
                while done < count:
                    codes, plane, j, left = h_mx[b, first + done]
                    width = min(left, count - done)
                    passes.append((b, done, width, codes[:, j : j + width], plane[:, j : j + width]))
                    done = done + width
            for number, (b, start, width, codes, plane) in enumerate(passes):
                nc.tensor.matmul_mx(
                    out=bank[:, start : start + width],
                    lhsT=w3_mx[n, b][0].bitcast(E4M3),
                    lhsT_scale=w3_mx[n, b][1],
                    rhs=codes.bitcast(E4M3),
                    rhs_scale=plane,
                    start=(number == 0),
                    stop=(number == len(passes) - 1),
                )
            y = work([P, count], F32, "y_sb%d_%d" % (n, first))
            nc.scalar.copy(out=y[:], in_=bank[:])
            nc.vector.tensor_tensor(
                pages[n][:].indirect(list_cols(idx2, first, count)), y[:], gains[:, first : first + count], ALU.mult
            )
            if first + count == S:
                nc.sync.dma_start(out=out[P * n : P * (n + 1), :], in_=pages[n][:])

        V, G = nc.vector, nc.gpsimd
        both = (0, HALF)

        def weigh_both(b, t):
            for first in both:
                weigh(b, t, first, HALF)
                finish(b, t, first, HALF, G)

        def weigh_half(b, t, first):
            weigh(b, t, first, HALF)
            finish(b, t, first, HALF, G)

        pick_words(0)
        pick_planes()
        weave_wa(0, 0, load_wa(0, 0))
        load_tab1()
        pick_words(1)
        quantise_wa(0, 0)
        weave_wa_shared(0, 1, load_wa(0, 1), "after_wa01")
        load_wb(0)
        order_wb_plane(0, V)
        order_wb(0, V)
        quantise_wa(0, 1)
        load_s(0, 0)
        pick(0, 0, 0, S)
        rest(0, 0, 0, S)
        order_wb_plane(1, G, "after_wa01")
        load_s(0, 1)
        pick(0, 1, 0, S)
        rest(0, 1, 0, S)
        load_wb(1)
        order_wb(1, G)
        weigh_both(0, 0)
        weigh_both(0, 1)
        load_s(0, 2)
        pick(0, 2, 0, S)
        raw = load_wa(1, 0)
        weigh_both(0, 2)
        weave_wa(1, 0, raw)
        load_s(0, 3)
        pick(0, 3, 0, S)
        quantise_wa(1, 0)
        weave_wa(1, 1, load_wa(1, 1))
        weigh_both(0, 3)
        load_s(1, 0)
        pick(1, 0, 0, S)
        quantise_wa(1, 1)
        weave_h(0, 0, HALF)
        rest(1, 0, 0, S)
        load_s(1, 1)
        pick(1, 1, 0, HALF)
        weigh(1, 0, 0, HALF)
        quantise_h(0, 0, HALF)
        finish(1, 0, 0, HALF, G)
        weigh_half(1, 0, HALF)
        weave_h(0, HALF, HALF)
        load_s(1, 2)
        rest(1, 1, 0, HALF)
        pick(1, 2, 0, HALF)
        rest(1, 2, 0, HALF)
        weigh_half(1, 1, 0)
        load_s(1, 3)
        gains = stream([P, S], F32, "gains")
        nc.sync.dma_start(out=gains[:], in_=wgo)
        load_w3(0)
        load_w3(1)
        idx2 = lists.tile([P, LIST_COLS], U16, name="idx2", tag="late_list", bufs=2, align_bytes=64)
        nc.sync.dma_start(idx2[:], offs2)
        pick(1, 3, 0, HALF)
        rest(1, 3, 0, HALF)
        weigh_half(1, 2, 0)
        pick(1, 1, HALF, HALF)
        weigh_half(1, 3, 0)
        rest(1, 1, HALF, HALF)
        weave_w3(0)
        pick(1, 2, HALF, HALF)
        rest(1, 2, HALF, HALF)
        weave_h(1, 0, QUARTER)
        weigh_half(1, 1, HALF)
        weigh_half(1, 2, HALF)
        weave_h(1, QUARTER, QUARTER)
        pick(1, 3, HALF, HALF)
        weigh(1, 3, HALF, HALF)
        quantise_w3(0)
        quantise_h(1, 0, QUARTER)
        weave_w3(1)
        quantise_h(1, QUARTER, QUARTER)
        finish(1, 3, HALF, HALF, V)
        quantise_h(0, HALF, HALF)
        quantise_w3(1)
        audit(0, 0, QUARTER)
        weave_w3(2)
        audit(0, QUARTER, QUARTER)
        quantise_w3(2)
        audit(1, 0, HALF)
        weave_w3(3)
        weave_h(1, HALF, HALF)
        audit(2, 0, HALF)
        quantise_w3(3)
        quantise_h(1, HALF, HALF)
        audit(3, 0, HALF)
        for n in range(N // P):
            audit(n, HALF, HALF)
